import numpy as np
import ml_dtypes


def mxq(x, axis, fmt="e4m3"):
    dtype, down = {"e4m3": (ml_dtypes.float8_e4m3fn, 7), "e5m2": (ml_dtypes.float8_e5m2, 14)}[fmt]
    v = np.moveaxis(np.asarray(x, np.float32).astype(ml_dtypes.bfloat16).astype(np.float64), axis, -1)
    blocks = v.reshape(v.shape[:-1] + (-1, 32))
    amax = np.abs(blocks).max(-1, keepdims=True)
    byte = np.maximum(np.where(amax > 0, np.frexp(amax)[1] - 1 + 127, 0) - down, 1)
    scale = np.exp2(byte - 127.0)
    codes = (blocks / scale).astype(np.float32).astype(dtype).astype(np.float64)
    return np.moveaxis((codes * scale).reshape(v.shape), -1, axis)


WIDE = False


def mx_kscale(k):
    if not WIDE:
        return np.ones(k)
    levels = np.array([10, -10, 5, -5, 0])
    if k % 512:
        return np.exp2(np.random.permutation(np.resize(levels, k // 32))).repeat(32)
    a = np.empty((k // 512, 16))
    for p in range(k // 512):
        a[p, :8] = np.random.permutation(np.resize(levels, 8))
        for g in range(8):
            far = levels[np.abs(levels - a[p, g]) >= 10]
            a[p, g + 8] = far[np.random.randint(len(far))]
    return np.exp2(a.ravel()).repeat(32)


def f64(x):
    return np.asarray(x).astype(np.float64)


def striped(idx):
    return np.tile(idx.reshape(-1, 16).T, (8, 1)).astype(np.uint16)


def unstriped(offs):
    return offs[:16].T.reshape(-1).astype(np.int64)


def gelu(v):
    return 0.5 * v * (1.0 + np.tanh(np.sqrt(2.0 / np.pi) * (v + 0.044715 * v**3)))


K, T, S, V, N = 1024, 1024, 512, 256, 256
P = 2 ** 7


def setup_inputs():
    n = np.random.standard_normal
    s = mx_kscale(K)[:, None]
    return {
        "xT": (n((K, T)) * s).astype(np.float32),
        "w1": (n((K, N)) / np.sqrt(K) / s).astype(np.float32),
        "frac": np.tile(np.random.uniform(0.05, 0.95, V), (P, 1)).astype(np.float32),
        "offs": striped(np.random.permutation(T)[:S]),
        "left": striped(np.random.permutation(S)[:V]),
        "right": striped(np.random.permutation(S)[:V]),
    }


def reference(xT, w1, frac, offs, left, right):
    xq = mxq(f64(xT)[:, unstriped(offs)], 0, "e4m3")
    y = gelu(mxq(f64(w1), 0, "e4m3").T @ xq)
    l = y[:, unstriped(left)]
    return l + (y[:, unstriped(right)] - l) * f64(frac)[:1]

@@ -1,0 +1,171 @@
+from contextlib import ExitStack
+
+import concourse.mybir as mybir
+
+K, T, S, V, N = 1024, 1024, 512, 256, 256
+FLOPS = 2 * K * S * N
+
+F32 = mybir.dt.float32
+BF16 = mybir.dt.bfloat16
+U32 = mybir.dt.uint32
+U16 = mybir.dt.uint16
+U8 = mybir.dt.uint8
+FP8X4 = mybir.dt.float8_e4m3fn_x4
+ACT = mybir.ActivationFunctionType
+ALU = mybir.AluOpType
+
+P = 128
+PACK = 4
+K_PASS = P * PACK
+CHUNKS = ((0, 0, 512, 256), (0, 512, 256, 128), (0, 768, 256, 128), (1, 0, 256, 0), (1, 256, 256, 128), (1, 512, 256, 128), (1, 768, 128, 0), (1, 896, 128, 128))
+SCALE_ROW = (4, 0)
+HALF = S // 2
+
+
+def interleave(copy, dst, src):
+    copy(dst.rearrange("p (c i) t -> p c t i", i=4), src.rearrange("p t (c i) -> p c t i", i=4))
+
+
+def tile_picked_lerp_gelu_e_kernel(tc, xT, w1, frac, offs, left, right, out):
+    nc = tc.nc
+    with ExitStack() as ctx:
+        keep = ctx.enter_context(tc.tile_pool(name="keep", bufs=1))
+        psum = ctx.enter_context(tc.psum_pool(name="psum", bufs=1))
+
+        offs_sb = keep.tile([P, S // 16], U16, name="offs_sb")
+        left_sb = keep.tile([P, V // 16], U16, name="left_sb")
+        right_sb = keep.tile([P, V // 16], U16, name="right_sb")
+
+        warm = keep.tile([P, 8], F32, name="warm")
+        warm_out = keep.tile([P, 8], F32, name="warm_out")
+        nc.vector.memset(warm[:], 0.0)
+        nc.scalar.activation(warm_out[:], warm[:], ACT.Gelu_apprx_tanh)
+
+        x_scales = keep.tile([P, T], U8, name="x_scales", align_bytes=64)
+        nc.gpsimd.memset(x_scales[:], 0)
+
+        x_raw = []
+        for c, (z, t0, n, nv) in enumerate(CHUNKS):
+            raw = keep.tile([P, PACK, n], F32, name="x_raw%d" % c)
+            rows = xT[z * K_PASS : (z + 1) * K_PASS, t0 : t0 + n]
+            nc.sync.dma_start(raw[:], rows.rearrange("(p j) t -> p j t", j=PACK))
+            x_raw.append(raw)
+            if c == 1:
+                nc.sync.dma_start(offs_sb[:], offs)
+        frac_sb = keep.tile([P, V], F32, name="frac_sb")
+        nc.sync.dma_start(frac_sb[:], frac)
+        w_raw = {}
+        raw = keep.tile([P, PACK, N], F32, name="w_raw0")
+        nc.sync.dma_start(raw[:], w1[0:K_PASS, :].rearrange("(p j) m -> p j m", j=PACK))
+        w_raw[0, 0] = raw[:, :, 0:P]
+        w_raw[0, 1] = raw[:, :, P:N]
+        for m in range(2):
+            raw = keep.tile([P, PACK, P], F32, name="w_raw1%d" % m, tag="slot01" if m == 0 else "raw11", align_bytes=64)
+            nc.sync.dma_start(raw[:], w1[K_PASS:K, m * P : (m + 1) * P].rearrange("(p j) m -> p j m", j=PACK))
+            w_raw[1, m] = raw[:]
+        nc.sync.dma_start(right_sb[:], right)
+        nc.sync.dma_start(left_sb[:], left)
+
+        x_words = [keep.tile([P, T], U32, name="x_words%d" % z, align_bytes=64) for z in range(2)]
+        picked0 = keep.tile([P, S], U32, name="picked0", align_bytes=64)
+        picked_scales = keep.tile([P, S], U8, name="picked_scales", align_bytes=64)
+
+        def round_chunk(c):
+            z, t0, n, nv = CHUNKS[c]
+            grouped = keep.tile([P, n, PACK], BF16, name="x_bf%d" % c, align_bytes=64)
+            if nv > 0:
+                interleave(nc.vector.tensor_copy, grouped[:, 0:nv, :], x_raw[c][:, :, 0:nv])
+            if nv < n:
+                interleave(nc.scalar.copy, grouped[:, nv:n, :], x_raw[c][:, :, nv:n])
+            return grouped
+
+        def quantize_chunk(c, grouped):
+            z, t0, n, nv = CHUNKS[c]
+            nc.vector.quantize_mx(
+                out=x_words[z][:, t0 : t0 + n].bitcast(FP8X4),
+                scales=x_scales[SCALE_ROW[z] : P, t0 : t0 + n],
+                in_=grouped[:].rearrange("p c t -> p (c t)"),
+            )
+
+        last = len(CHUNKS) - 1
+        held = None
+        for c in range(len(CHUNKS)):
+            grouped = round_chunk(c)
+            if held is not None:
+                quantize_chunk(c - 1, held)
+                held = None
+            if c == last - 1:
+                held = grouped
+            else:
+                quantize_chunk(c, grouped)
+            if CHUNKS[c][0] == 0 and CHUNKS[c + 1][0] == 1:
+                nc.vector.tensor_copy(picked0[:], x_words[0][:].indirect(offs_sb[:]))
+
+        w_words = {}
+        w_scales = {}
+        w_bf = {}
+
+        def round_w(z, m):
+            w_bf[z, m] = keep.tile([P, P, PACK], BF16, name="w_bf%d%d" % (z, m), tag="slot%d%d" % (z, m), align_bytes=64)
+            interleave(nc.scalar.copy, w_bf[z, m][:], w_raw[z, m])
+
+        def quantize_w(z, m):
+            w_words[z, m] = keep.tile([P, P], U32, name="w_words%d%d" % (z, m), align_bytes=64)
+            w_scales[z, m] = keep.tile([P, P], U8, name="w_scales%d%d" % (z, m), align_bytes=64)
+            nc.vector.quantize_mx(
+                out=w_words[z, m][:].bitcast(FP8X4),
+                scales=w_scales[z, m][:],
+                in_=w_bf[z, m][:].rearrange("p c t -> p (c t)"),
+            )
+
+        y = [keep.tile([P, S], F32, name="y%d" % m) for m in range(2)]
+
+        acc = {(m, h): psum.tile([P, HALF], F32, name="acc%d%d" % (m, h)) for m in range(2) for h in range(2)}
+
+        def product(z, m, h):
+            cols = slice(h * HALF, (h + 1) * HALF)
+            words = picked0[:, cols] if z == 0 else picked1[h][:]
+            nc.tensor.matmul_mx(
+                out=acc[m, h][:],
+                lhsT=w_words[z, m][:].bitcast(FP8X4),
+                lhsT_scale=w_scales[z, m][:],
+                rhs=words.bitcast(FP8X4),
+                rhs_scale=picked_scales[SCALE_ROW[z] : P, cols],
+                start=(z == 0),
+                stop=(z == 1),
+            )
+            if z == 1:
+                nc.scalar.activation(y[m][:, cols], acc[m, h][:], ACT.Gelu_apprx_tanh)
+
+        rest = keep.tile([P, V], F32, name="rest")
+        nc.scalar.activation(rest[:], frac_sb[:], ACT.Copy, bias=1.0, scale=-1.0)
+        round_w(0, 0)
+        round_w(1, 0)
+        round_w(0, 1)
+        round_w(1, 1)
+
+        nc.vector.tensor_copy(picked_scales[:], x_scales[:].indirect(offs_sb[:]))
+        quantize_w(0, 0)
+        picked1 = [keep.tile([P, HALF], U32, name="picked10", tag="slot00", align_bytes=64)]
+        nc.vector.tensor_copy(picked1[0][:], x_words[1][:].indirect(offs_sb[:, 0 : HALF // 16]))
+        quantize_w(1, 0)
+        product(0, 0, 0)
+        product(0, 0, 1)
+        product(1, 0, 0)
+        picked1.append(keep.tile([P, HALF], U32, name="picked11", tag="slot10", align_bytes=64))
+        nc.vector.tensor_copy(picked1[1][:], x_words[1][:].indirect(offs_sb[:, HALF // 16 : S // 16]))
+        product(1, 0, 1)
+        quantize_w(0, 1)
+        quantize_w(1, 1)
+        for h in range(2):
+            product(0, 1, h)
+            product(1, 1, h)
+
+        for m in range(2):
+            from_left = keep.tile([P, V], F32, name="from_left%d" % m)
+            from_right = keep.tile([P, V], F32, name="from_right%d" % m, tag="slot11" if m == 0 else "last", align_bytes=64)
+            result = keep.tile([P, V], F32, name="result%d" % m)
+            nc.vector.tensor_tensor(from_right[:], y[m][:].indirect(right_sb[:]), frac_sb[:], ALU.mult)
+            nc.vector.tensor_tensor(from_left[:], y[m][:].indirect(left_sb[:]), rest[:], ALU.mult)
+            nc.vector.tensor_tensor(result[:], from_left[:], from_right[:], ALU.add)
+            nc.sync.dma_start(out[m * P : (m + 1) * P, :], result[:])

@@ -17,7 +17,7 @@ ALU = mybir.AluOpType
 P = 128
 PACK = 4
 K_PASS = P * PACK
-CHUNKS = ((0, 0, 512, 256), (0, 512, 256, 128), (0, 768, 256, 128), (1, 0, 256, 0), (1, 256, 256, 128), (1, 512, 256, 128), (1, 768, 128, 0), (1, 896, 128, 128))
+CHUNKS = ((0, 0, 512, 320), (0, 512, 512, 320), (1, 0, 512, 192), (1, 512, 256, 160), (1, 768, 256, 160))
 SCALE_ROW = (4, 0)
 HALF = S // 2
 
@@ -52,17 +52,14 @@ def tile_picked_lerp_gelu_e_kernel(tc, xT, w1, frac, offs, left, right, out):
             x_raw.append(raw)
             if c == 1:
                 nc.sync.dma_start(offs_sb[:], offs)
+        w_raw = {}
+        for z in range(2):
+            raw = keep.tile([P, PACK, N], F32, name="w_raw%d" % z)
+            nc.sync.dma_start(raw[:], w1[z * K_PASS : (z + 1) * K_PASS, :].rearrange("(p j) m -> p j m", j=PACK))
+            w_raw[z, 0] = raw[:, :, 0:P]
+            w_raw[z, 1] = raw[:, :, P:N]
         frac_sb = keep.tile([P, V], F32, name="frac_sb")
         nc.sync.dma_start(frac_sb[:], frac)
-        w_raw = {}
-        raw = keep.tile([P, PACK, N], F32, name="w_raw0")
-        nc.sync.dma_start(raw[:], w1[0:K_PASS, :].rearrange("(p j) m -> p j m", j=PACK))
-        w_raw[0, 0] = raw[:, :, 0:P]
-        w_raw[0, 1] = raw[:, :, P:N]
-        for m in range(2):
-            raw = keep.tile([P, PACK, P], F32, name="w_raw1%d" % m, tag="slot01" if m == 0 else "raw11", align_bytes=64)
-            nc.sync.dma_start(raw[:], w1[K_PASS:K, m * P : (m + 1) * P].rearrange("(p j) m -> p j m", j=PACK))
-            w_raw[1, m] = raw[:]
         nc.sync.dma_start(right_sb[:], right)
         nc.sync.dma_start(left_sb[:], left)
 
@@ -87,18 +84,9 @@ def tile_picked_lerp_gelu_e_kernel(tc, xT, w1, frac, offs, left, right, out):
                 in_=grouped[:].rearrange("p c t -> p (c t)"),
             )
 
-        last = len(CHUNKS) - 1
-        held = None
         for c in range(len(CHUNKS)):
-            grouped = round_chunk(c)
-            if held is not None:
-                quantize_chunk(c - 1, held)
-                held = None
-            if c == last - 1:
-                held = grouped
-            else:
-                quantize_chunk(c, grouped)
-            if CHUNKS[c][0] == 0 and CHUNKS[c + 1][0] == 1:
+            quantize_chunk(c, round_chunk(c))
+            if c == 1:
                 nc.vector.tensor_copy(picked0[:], x_words[0][:].indirect(offs_sb[:]))
 
         w_words = {}
@@ -137,11 +125,9 @@ def tile_picked_lerp_gelu_e_kernel(tc, xT, w1, frac, offs, left, right, out):
             if z == 1:
                 nc.scalar.activation(y[m][:, cols], acc[m, h][:], ACT.Gelu_apprx_tanh)
 
-        rest = keep.tile([P, V], F32, name="rest")
-        nc.scalar.activation(rest[:], frac_sb[:], ACT.Copy, bias=1.0, scale=-1.0)
         round_w(0, 0)
-        round_w(1, 0)
         round_w(0, 1)
+        round_w(1, 0)
         round_w(1, 1)
 
         nc.vector.tensor_copy(picked_scales[:], x_scales[:].indirect(offs_sb[:]))
@@ -155,6 +141,8 @@ def tile_picked_lerp_gelu_e_kernel(tc, xT, w1, frac, offs, left, right, out):
         picked1.append(keep.tile([P, HALF], U32, name="picked11", tag="slot10", align_bytes=64))
         nc.vector.tensor_copy(picked1[1][:], x_words[1][:].indirect(offs_sb[:, HALF // 16 : S // 16]))
         product(1, 0, 1)
+        rest = keep.tile([P, V], F32, name="rest")
+        nc.vector.tensor_scalar(rest[:], frac_sb[:], -1.0, 1.0, ALU.mult, ALU.add)
         quantize_w(0, 1)
         quantize_w(1, 1)
         for h in range(2):

@@ -17,9 +17,8 @@ ALU = mybir.AluOpType
 P = 128
 PACK = 4
 K_PASS = P * PACK
-CHUNKS = ((0, 0, 512, 320), (0, 512, 512, 320), (1, 0, 512, 192), (1, 512, 256, 160), (1, 768, 256, 160))
-SCALE_ROW = (4, 0)
 HALF = S // 2
+LAST_PIECES = (slice(0, 256), slice(256, 384), slice(384, S))
 
 
 def interleave(copy, dst, src):
@@ -41,17 +40,14 @@ def tile_picked_lerp_gelu_e_kernel(tc, xT, w1, frac, offs, left, right, out):
         nc.vector.memset(warm[:], 0.0)
         nc.scalar.activation(warm_out[:], warm[:], ACT.Gelu_apprx_tanh)
 
-        x_scales = keep.tile([P, T], U8, name="x_scales", align_bytes=64)
-        nc.gpsimd.memset(x_scales[:], 0)
-
-        x_raw = []
-        for c, (z, t0, n, nv) in enumerate(CHUNKS):
-            raw = keep.tile([P, PACK, n], F32, name="x_raw%d" % c)
-            rows = xT[z * K_PASS : (z + 1) * K_PASS, t0 : t0 + n]
-            nc.sync.dma_start(raw[:], rows.rearrange("(p j) t -> p j t", j=PACK))
-            x_raw.append(raw)
-            if c == 1:
-                nc.sync.dma_start(offs_sb[:], offs)
+        x_rows = xT.rearrange("(z p j) t -> z j p t", p=P, j=PACK)
+        x_raw = {}
+        for z in range(2):
+            for j in range(PACK):
+                x_raw[z, j] = keep.tile([P, T], F32, name="x_raw%d%d" % (z, j), align_bytes=64)
+                nc.sync.dma_start(x_raw[z, j][:], x_rows[z, j])
+                if (z, j) == (0, 0):
+                    nc.sync.dma_start(offs_sb[:], offs)
         w_raw = {}
         for z in range(2):
             raw = keep.tile([P, PACK, N], F32, name="w_raw%d" % z)
@@ -63,97 +59,106 @@ def tile_picked_lerp_gelu_e_kernel(tc, xT, w1, frac, offs, left, right, out):
         nc.sync.dma_start(right_sb[:], right)
         nc.sync.dma_start(left_sb[:], left)
 
-        x_words = [keep.tile([P, T], U32, name="x_words%d" % z, align_bytes=64) for z in range(2)]
-        picked0 = keep.tile([P, S], U32, name="picked0", align_bytes=64)
-        picked_scales = keep.tile([P, S], U8, name="picked_scales", align_bytes=64)
+        picked = [keep.tile([P, PACK, S], F32, name="picked%d" % z) for z in range(2)]
+        halves = [slice(h * HALF, (h + 1) * HALF) for h in range(2)]
 
-        def round_chunk(c):
-            z, t0, n, nv = CHUNKS[c]
-            grouped = keep.tile([P, n, PACK], BF16, name="x_bf%d" % c, align_bytes=64)
-            if nv > 0:
-                interleave(nc.vector.tensor_copy, grouped[:, 0:nv, :], x_raw[c][:, :, 0:nv])
-            if nv < n:
-                interleave(nc.scalar.copy, grouped[:, nv:n, :], x_raw[c][:, :, nv:n])
-            return grouped
-
-        def quantize_chunk(c, grouped):
-            z, t0, n, nv = CHUNKS[c]
+        def quantize(name, grouped, n, tag=None):
+            words = keep.tile([P, n], U32, name=name + "_words", tag=tag or name + "_words", align_bytes=64)
+            scales = keep.tile([P, n], U8, name=name + "_scales", align_bytes=64)
             nc.vector.quantize_mx(
-                out=x_words[z][:, t0 : t0 + n].bitcast(FP8X4),
-                scales=x_scales[SCALE_ROW[z] : P, t0 : t0 + n],
-                in_=grouped[:].rearrange("p c t -> p (c t)"),
+                out=words[:].bitcast(FP8X4), scales=scales[:], in_=grouped.rearrange("p c t -> p (c t)")
             )
+            return words, scales
 
-        for c in range(len(CHUNKS)):
-            quantize_chunk(c, round_chunk(c))
-            if c == 1:
-                nc.vector.tensor_copy(picked0[:], x_words[0][:].indirect(offs_sb[:]))
-
-        w_words = {}
-        w_scales = {}
-        w_bf = {}
-
-        def round_w(z, m):
-            w_bf[z, m] = keep.tile([P, P, PACK], BF16, name="w_bf%d%d" % (z, m), tag="slot%d%d" % (z, m), align_bytes=64)
-            interleave(nc.scalar.copy, w_bf[z, m][:], w_raw[z, m])
-
-        def quantize_w(z, m):
-            w_words[z, m] = keep.tile([P, P], U32, name="w_words%d%d" % (z, m), align_bytes=64)
-            w_scales[z, m] = keep.tile([P, P], U8, name="w_scales%d%d" % (z, m), align_bytes=64)
-            nc.vector.quantize_mx(
-                out=w_words[z, m][:].bitcast(FP8X4),
-                scales=w_scales[z, m][:],
-                in_=w_bf[z, m][:].rearrange("p c t -> p (c t)"),
+        for j in range(PACK):
+            nc.vector.tensor_copy(picked[0][:, j, :], x_raw[0, j][:].indirect(offs_sb[:]))
+        x_bf0 = keep.tile([P, S, PACK], BF16, name="x_bf0", align_bytes=64)
+        interleave(nc.scalar.copy, x_bf0[:], picked[0][:])
+        for j in range(PACK - 1):
+            nc.vector.tensor_copy(picked[1][:, j, :], x_raw[1, j][:].indirect(offs_sb[:]))
+        x_bf1 = keep.tile([P, S, PACK], BF16, name="x_bf1", align_bytes=64)
+        for piece in LAST_PIECES:
+            nc.vector.tensor_copy(
+                picked[1][:, PACK - 1, piece],
+                x_raw[1, PACK - 1][:].indirect(offs_sb[:, piece.start // 16 : piece.stop // 16]),
             )
+        interleave(nc.scalar.copy, x_bf1[:, LAST_PIECES[0], :], picked[1][:, :, LAST_PIECES[0]])
+        interleave(nc.scalar.copy, x_bf1[:, LAST_PIECES[2], :], picked[1][:, :, LAST_PIECES[2]])
+        w_bf_low = [keep.tile([P, P, PACK], BF16, name="w_bf_low%d" % z, align_bytes=64) for z in range(2)]
+        interleave(nc.scalar.copy, w_bf_low[1][:], w_raw[1, 0])
+        rest = keep.tile([P, V], F32, name="rest")
+        nc.scalar.activation(rest[:], frac_sb[:], ACT.Copy, bias=1.0, scale=-1.0)
 
         y = [keep.tile([P, S], F32, name="y%d" % m) for m in range(2)]
-
         acc = {(m, h): psum.tile([P, HALF], F32, name="acc%d%d" % (m, h)) for m in range(2) for h in range(2)}
+        x_mx = {}
+        w_mx = {}
 
         def product(z, m, h):
-            cols = slice(h * HALF, (h + 1) * HALF)
-            words = picked0[:, cols] if z == 0 else picked1[h][:]
             nc.tensor.matmul_mx(
                 out=acc[m, h][:],
-                lhsT=w_words[z, m][:].bitcast(FP8X4),
-                lhsT_scale=w_scales[z, m][:],
-                rhs=words.bitcast(FP8X4),
-                rhs_scale=picked_scales[SCALE_ROW[z] : P, cols],
+                lhsT=w_mx[z, m][0].bitcast(FP8X4),
+                lhsT_scale=w_mx[z, m][1],
+                rhs=x_mx[z, h][0].bitcast(FP8X4),
+                rhs_scale=x_mx[z, h][1],
                 start=(z == 0),
                 stop=(z == 1),
             )
             if z == 1:
-                nc.scalar.activation(y[m][:, cols], acc[m, h][:], ACT.Gelu_apprx_tanh)
+                nc.scalar.activation(y[m][:, halves[h]], acc[m, h][:], ACT.Gelu_apprx_tanh)
 
-        round_w(0, 0)
-        round_w(0, 1)
-        round_w(1, 0)
-        round_w(1, 1)
-
-        nc.vector.tensor_copy(picked_scales[:], x_scales[:].indirect(offs_sb[:]))
-        quantize_w(0, 0)
-        picked1 = [keep.tile([P, HALF], U32, name="picked10", tag="slot00", align_bytes=64)]
-        nc.vector.tensor_copy(picked1[0][:], x_words[1][:].indirect(offs_sb[:, 0 : HALF // 16]))
-        quantize_w(1, 0)
+        interleave(nc.vector.tensor_copy, x_bf1[:, LAST_PIECES[1], :], picked[1][:, :, LAST_PIECES[1]])
+        words, scales = quantize("x0", x_bf0[:], S, tag="x_raw13")
+        for h in range(2):
+            x_mx[0, h] = (words[:, halves[h]], scales[:, halves[h]])
+        interleave(nc.vector.tensor_copy, w_bf_low[0][:], w_raw[0, 0])
+        words, scales = quantize("x10", x_bf1[:, halves[0], :], HALF)
+        x_mx[1, 0] = (words[:], scales[:])
+        words, scales = quantize("w00", w_bf_low[0][:], P)
+        w_mx[0, 0] = (words[:], scales[:])
         product(0, 0, 0)
         product(0, 0, 1)
+        words, scales = quantize("x11", x_bf1[:, halves[1], :], HALF)
+        x_mx[1, 1] = (words[:], scales[:])
+        words, scales = quantize("w10", w_bf_low[1][:], P)
+        w_mx[1, 0] = (words[:], scales[:])
         product(1, 0, 0)
-        picked1.append(keep.tile([P, HALF], U32, name="picked11", tag="slot10", align_bytes=64))
-        nc.vector.tensor_copy(picked1[1][:], x_words[1][:].indirect(offs_sb[:, HALF // 16 : S // 16]))
         product(1, 0, 1)
-        rest = keep.tile([P, V], F32, name="rest")
-        nc.vector.tensor_scalar(rest[:], frac_sb[:], -1.0, 1.0, ALU.mult, ALU.add)
-        quantize_w(0, 1)
-        quantize_w(1, 1)
-        for h in range(2):
-            product(0, 1, h)
-            product(1, 1, h)
 
-        for m in range(2):
-            from_left = keep.tile([P, V], F32, name="from_left%d" % m)
-            from_right = keep.tile([P, V], F32, name="from_right%d" % m, tag="slot11" if m == 0 else "last", align_bytes=64)
-            result = keep.tile([P, V], F32, name="result%d" % m)
-            nc.vector.tensor_tensor(from_right[:], y[m][:].indirect(right_sb[:]), frac_sb[:], ALU.mult)
-            nc.vector.tensor_tensor(from_left[:], y[m][:].indirect(left_sb[:]), rest[:], ALU.mult)
-            nc.vector.tensor_tensor(result[:], from_left[:], from_right[:], ALU.add)
-            nc.sync.dma_start(out[m * P : (m + 1) * P, :], result[:])
+        w_bf_high = []
+        for z, copy, tag in ((0, nc.scalar.copy, "x_bf1"), (1, nc.vector.tensor_copy, "w_bf_low1")):
+            w_bf_high.append(keep.tile([P, P, PACK], BF16, name="w_bf_high%d" % z, tag=tag, align_bytes=64))
+            interleave(copy, w_bf_high[z][:], w_raw[z, 1])
+        for z in range(2):
+            words, scales = quantize("w_high%d" % z, w_bf_high[z][:], P)
+            w_mx[z, 1] = (words[:], scales[:])
+        for z in range(2):
+            for h in range(2):
+                product(z, 1, h)
+
+        from_right = [
+            keep.tile([P, V], F32, name="from_right0", tag="w_bf_low1", align_bytes=64),
+            keep.tile([P, V], F32, name="from_right1"),
+        ]
+        from_left = [
+            keep.tile([P, V], F32, name="from_left0", tag="x_bf1", align_bytes=64),
+            keep.tile([P, V], F32, name="from_left1"),
+        ]
+        nc.vector.tensor_tensor(from_right[0][:], y[0][:].indirect(right_sb[:]), frac_sb[:], ALU.mult)
+        nc.vector.tensor_tensor(from_left[0][:], y[0][:].indirect(left_sb[:]), rest[:], ALU.mult)
+        nc.vector.tensor_tensor(from_right[1][:], y[1][:].indirect(right_sb[:]), frac_sb[:], ALU.mult)
+        samples = [slice(0, V // 2), slice(V // 2, V)]
+
+        def last_left(part):
+            picks = left_sb[:, part.start // 16 : part.stop // 16]
+            nc.vector.tensor_tensor(from_left[1][:, part], y[1][:].indirect(picks), rest[:, part], ALU.mult)
+
+        last_left(samples[0])
+        result0 = keep.tile([P, V], F32, name="result0", tag="frac_sb")
+        nc.vector.tensor_tensor(result0[:], from_left[0][:], from_right[0][:], ALU.add)
+        nc.sync.dma_start(out[0:P, :], result0[:])
+        last_left(samples[1])
+        result1 = keep.tile([P, V], F32, name="result1")
+        for part in samples:
+            nc.vector.tensor_tensor(result1[:, part], from_left[1][:, part], from_right[1][:, part], ALU.add)
+        nc.sync.dma_start(out[P:N, :], result1[:])

@@ -8,6 +8,7 @@ FLOPS = 2 * K * S * N
 F32 = mybir.dt.float32
 BF16 = mybir.dt.bfloat16
 U32 = mybir.dt.uint32
+I32 = mybir.dt.int32
 U16 = mybir.dt.uint16
 U8 = mybir.dt.uint8
 FP8X4 = mybir.dt.float8_e4m3fn_x4
@@ -18,7 +19,9 @@ P = 128
 PACK = 4
 K_PASS = P * PACK
 HALF = S // 2
-LAST_PIECES = (slice(0, 256), slice(256, 384), slice(384, S))
+PAIR_LOADS = ((0, 0, T), (1, 0, T // 2), (1, T // 2, T))
+FIRST_SPLIT = 368
+LAST_SPLIT = 304
 
 
 def interleave(copy, dst, src):
@@ -40,17 +43,20 @@ def tile_picked_lerp_gelu_e_kernel(tc, xT, w1, frac, offs, left, right, out):
         nc.vector.memset(warm[:], 0.0)
         nc.scalar.activation(warm_out[:], warm[:], ACT.Gelu_apprx_tanh)
 
-        x_rows = xT.rearrange("(z p j) t -> z j p t", p=P, j=PACK)
-        x_raw = {}
-        for z in range(2):
-            for j in range(PACK):
-                x_raw[z, j] = keep.tile([P, T], F32, name="x_raw%d%d" % (z, j), align_bytes=64)
-                nc.sync.dma_start(x_raw[z, j][:], x_rows[z, j])
-                if (z, j) == (0, 0):
-                    nc.sync.dma_start(offs_sb[:], offs)
+        x_rows = xT.rearrange("(z p j) t -> z p j t", p=P, j=PACK)
+        x_plane = []
+        for j in range(PACK):
+            x_plane.append(keep.tile([P, T], F32, name="x_plane%d" % j, align_bytes=64))
+            nc.sync.dma_start(x_plane[j][:], x_rows[0, :, j, :])
+            if j == 0:
+                nc.sync.dma_start(offs_sb[:], offs)
+        x_part = []
+        for u, first, last in PAIR_LOADS:
+            x_part.append(keep.tile([P, 2, last - first], F32, name="x_part%d" % len(x_part), align_bytes=64))
+            nc.sync.dma_start(x_part[-1][:], x_rows[1, :, 2 * u : 2 * u + 2, first:last])
         w_raw = {}
         for z in range(2):
-            raw = keep.tile([P, PACK, N], F32, name="w_raw%d" % z)
+            raw = keep.tile([P, PACK, N], F32, name="w_raw%d" % z, align_bytes=64)
             nc.sync.dma_start(raw[:], w1[z * K_PASS : (z + 1) * K_PASS, :].rearrange("(p j) m -> p j m", j=PACK))
             w_raw[z, 0] = raw[:, :, 0:P]
             w_raw[z, 1] = raw[:, :, P:N]
@@ -59,40 +65,62 @@ def tile_picked_lerp_gelu_e_kernel(tc, xT, w1, frac, offs, left, right, out):
         nc.sync.dma_start(right_sb[:], right)
         nc.sync.dma_start(left_sb[:], left)
 
-        picked = [keep.tile([P, PACK, S], F32, name="picked%d" % z) for z in range(2)]
         halves = [slice(h * HALF, (h + 1) * HALF) for h in range(2)]
 
-        def quantize(name, grouped, n, tag=None):
-            words = keep.tile([P, n], U32, name=name + "_words", tag=tag or name + "_words", align_bytes=64)
+        def quantize(name, grouped, n):
+            words = keep.tile([P, n], U32, name=name + "_words", align_bytes=64)
             scales = keep.tile([P, n], U8, name=name + "_scales", align_bytes=64)
-            nc.vector.quantize_mx(
-                out=words[:].bitcast(FP8X4), scales=scales[:], in_=grouped.rearrange("p c t -> p (c t)")
-            )
+            nc.vector.quantize_mx(out=words[:].bitcast(FP8X4), scales=scales[:], in_=grouped)
             return words, scales
 
+        x_mx = {}
+        w_mx = {}
+
+        picked = [keep.tile([P, 2, S], F32, name="picked%d" % u) for u in range(2)]
         for j in range(PACK):
-            nc.vector.tensor_copy(picked[0][:, j, :], x_raw[0, j][:].indirect(offs_sb[:]))
+            nc.vector.tensor_copy(picked[j // 2][:, j % 2, :], x_plane[j][:].indirect(offs_sb[:]))
         x_bf0 = keep.tile([P, S, PACK], BF16, name="x_bf0", align_bytes=64)
-        interleave(nc.scalar.copy, x_bf0[:], picked[0][:])
-        for j in range(PACK - 1):
-            nc.vector.tensor_copy(picked[1][:, j, :], x_raw[1, j][:].indirect(offs_sb[:]))
-        x_bf1 = keep.tile([P, S, PACK], BF16, name="x_bf1", align_bytes=64)
-        for piece in LAST_PIECES:
-            nc.vector.tensor_copy(
-                picked[1][:, PACK - 1, piece],
-                x_raw[1, PACK - 1][:].indirect(offs_sb[:, piece.start // 16 : piece.stop // 16]),
-            )
-        interleave(nc.scalar.copy, x_bf1[:, LAST_PIECES[0], :], picked[1][:, :, LAST_PIECES[0]])
-        interleave(nc.scalar.copy, x_bf1[:, LAST_PIECES[2], :], picked[1][:, :, LAST_PIECES[2]])
+        nc.scalar.copy(x_bf0[:, :, 0:2], picked[0][:].rearrange("p e c -> p c e"))
+        nc.vector.tensor_copy(x_bf0[:, :, 2:4], picked[1][:].rearrange("p e c -> p c e"))
+        words, scales = quantize("x0", x_bf0[:].rearrange("p c t -> p (c t)"), S)
+        for h in range(2):
+            x_mx[0, h] = (words[:, halves[h]], scales[:, halves[h]])
+
+        pairs = [keep.tile([P, T, 2], BF16, name="pairs%d" % u, align_bytes=64) for u in range(2)]
+
+        def pair_up(copy, part, first, last):
+            u, base = PAIR_LOADS[part][:2]
+            copy(pairs[u][:, base + first : base + last, :], x_part[part][:, :, first:last].rearrange("p e t -> p t e"))
+
+        got = [keep.tile([P, 2, HALF], U32, name="got%d" % h, align_bytes=64) for h in range(2)]
+
+        def pick_pairs(u):
+            window = pairs[u][:].rearrange("p t e -> p (t e)").bitcast(U32)
+            for h in range(2):
+                picks = offs_sb[:, h * (HALF // 16) : (h + 1) * (HALF // 16)]
+                nc.vector.tensor_copy(got[h][:, u, :], window.indirect(picks))
+
+        pair_up(nc.vector.tensor_copy, 0, 0, FIRST_SPLIT)
+        pair_up(nc.scalar.copy, 0, FIRST_SPLIT, T)
+        pick_pairs(0)
+        pair_up(nc.scalar.copy, 1, 0, T // 2)
+        pair_up(nc.vector.tensor_copy, 2, 0, LAST_SPLIT)
+        pair_up(nc.scalar.copy, 2, LAST_SPLIT, T // 2)
+        pick_pairs(1)
+        x_bf1 = [keep.tile([P, HALF, 2], I32, name="x_bf1%d" % h, align_bytes=64) for h in range(2)]
+        for h in range(2):
+            nc.vector.tensor_copy(x_bf1[h][:], got[h][:].bitcast(I32).rearrange("p u c -> p c u"))
+
         w_bf_low = [keep.tile([P, P, PACK], BF16, name="w_bf_low%d" % z, align_bytes=64) for z in range(2)]
-        interleave(nc.scalar.copy, w_bf_low[1][:], w_raw[1, 0])
+        w_bf_high = keep.tile([P, 2, P, PACK], BF16, name="w_bf_high", align_bytes=64)
+        for z in range(2):
+            interleave(nc.scalar.copy, w_bf_low[z][:], w_raw[z, 0])
+            interleave(nc.scalar.copy, w_bf_high[:, z], w_raw[z, 1])
         rest = keep.tile([P, V], F32, name="rest")
         nc.scalar.activation(rest[:], frac_sb[:], ACT.Copy, bias=1.0, scale=-1.0)
 
         y = [keep.tile([P, S], F32, name="y%d" % m) for m in range(2)]
         acc = {(m, h): psum.tile([P, HALF], F32, name="acc%d%d" % (m, h)) for m in range(2) for h in range(2)}
-        x_mx = {}
-        w_mx = {}
 
         def product(z, m, h):
             nc.tensor.matmul_mx(
@@ -107,41 +135,37 @@ def tile_picked_lerp_gelu_e_kernel(tc, xT, w1, frac, offs, left, right, out):
             if z == 1:
                 nc.scalar.activation(y[m][:, halves[h]], acc[m, h][:], ACT.Gelu_apprx_tanh)
 
-        interleave(nc.vector.tensor_copy, x_bf1[:, LAST_PIECES[1], :], picked[1][:, :, LAST_PIECES[1]])
-        words, scales = quantize("x0", x_bf0[:], S, tag="x_raw13")
-        for h in range(2):
-            x_mx[0, h] = (words[:, halves[h]], scales[:, halves[h]])
-        interleave(nc.vector.tensor_copy, w_bf_low[0][:], w_raw[0, 0])
-        words, scales = quantize("x10", x_bf1[:, halves[0], :], HALF)
-        x_mx[1, 0] = (words[:], scales[:])
-        words, scales = quantize("w00", w_bf_low[0][:], P)
+        words, scales = quantize("w00", w_bf_low[0][:].rearrange("p c t -> p (c t)"), P)
         w_mx[0, 0] = (words[:], scales[:])
         product(0, 0, 0)
         product(0, 0, 1)
-        words, scales = quantize("x11", x_bf1[:, halves[1], :], HALF)
-        x_mx[1, 1] = (words[:], scales[:])
-        words, scales = quantize("w10", w_bf_low[1][:], P)
+        x1_words = keep.tile([P, S], U32, name="x1_words", tag="w_raw0", align_bytes=64)
+        x1_scales = keep.tile([P, S], U8, name="x1_scales", align_bytes=64)
+        for h in range(2):
+            x_mx[1, h] = (x1_words[:, halves[h]], x1_scales[:, halves[h]])
+            nc.vector.quantize_mx(
+                out=x_mx[1, h][0].bitcast(FP8X4),
+                scales=x_mx[1, h][1],
+                in_=x_bf1[h][:].rearrange("p c u -> p (c u)").bitcast(BF16),
+            )
+        words, scales = quantize("w10", w_bf_low[1][:].rearrange("p c t -> p (c t)"), P)
         w_mx[1, 0] = (words[:], scales[:])
         product(1, 0, 0)
         product(1, 0, 1)
 
-        w_bf_high = []
-        for z, copy, tag in ((0, nc.scalar.copy, "x_bf1"), (1, nc.vector.tensor_copy, "w_bf_low1")):
-            w_bf_high.append(keep.tile([P, P, PACK], BF16, name="w_bf_high%d" % z, tag=tag, align_bytes=64))
-            interleave(copy, w_bf_high[z][:], w_raw[z, 1])
+        words, scales = quantize("w_high", w_bf_high[:].rearrange("p z c t -> p (z c t)"), 2 * P)
         for z in range(2):
-            words, scales = quantize("w_high%d" % z, w_bf_high[z][:], P)
-            w_mx[z, 1] = (words[:], scales[:])
+            w_mx[z, 1] = (words[:, z * P : (z + 1) * P], scales[:, z * P : (z + 1) * P])
         for z in range(2):
             for h in range(2):
                 product(z, 1, h)
 
         from_right = [
-            keep.tile([P, V], F32, name="from_right0", tag="w_bf_low1", align_bytes=64),
+            keep.tile([P, V], F32, name="from_right0"),
             keep.tile([P, V], F32, name="from_right1"),
         ]
         from_left = [
-            keep.tile([P, V], F32, name="from_left0", tag="x_bf1", align_bytes=64),
+            keep.tile([P, V], F32, name="from_left0"),
             keep.tile([P, V], F32, name="from_left1"),
         ]
         nc.vector.tensor_tensor(from_right[0][:], y[0][:].indirect(right_sb[:]), frac_sb[:], ALU.mult)

@@ -19,9 +19,8 @@ P = 128
 PACK = 4
 K_PASS = P * PACK
 HALF = S // 2
-PAIR_LOADS = ((0, 0, T), (1, 0, T // 2), (1, T // 2, T))
-FIRST_SPLIT = 368
-LAST_SPLIT = 304
+PAIR_LOADS = ((0, 0, T // 2), (0, T // 2, T), (1, 0, T // 2), (1, T // 2, T))
+LAST_SPLIT = 264
 
 
 def interleave(copy, dst, src):
@@ -76,15 +75,18 @@ def tile_picked_lerp_gelu_e_kernel(tc, xT, w1, frac, offs, left, right, out):
         x_mx = {}
         w_mx = {}
 
+        lists = [offs_sb[:, h * (HALF // 16) : (h + 1) * (HALF // 16)] for h in range(2)]
         picked = [keep.tile([P, 2, S], F32, name="picked%d" % u) for u in range(2)]
-        for j in range(PACK):
-            nc.vector.tensor_copy(picked[j // 2][:, j % 2, :], x_plane[j][:].indirect(offs_sb[:]))
-        x_bf0 = keep.tile([P, S, PACK], BF16, name="x_bf0", align_bytes=64)
-        nc.scalar.copy(x_bf0[:, :, 0:2], picked[0][:].rearrange("p e c -> p c e"))
-        nc.vector.tensor_copy(x_bf0[:, :, 2:4], picked[1][:].rearrange("p e c -> p c e"))
-        words, scales = quantize("x0", x_bf0[:].rearrange("p c t -> p (c t)"), S)
+        x_bf0 = [keep.tile([P, HALF, PACK], BF16, name="x_bf0%d" % h, align_bytes=64) for h in range(2)]
+        for u, copy in enumerate((nc.scalar.copy, nc.vector.tensor_copy)):
+            nc.vector.tensor_copy(picked[u][:, 0, :], x_plane[2 * u][:].indirect(offs_sb[:]))
+            for h in range(2):
+                nc.vector.tensor_copy(picked[u][:, 1, halves[h]], x_plane[2 * u + 1][:].indirect(lists[h]))
+            for h in range(2):
+                copy(x_bf0[h][:, :, 2 * u : 2 * u + 2], picked[u][:, :, halves[h]].rearrange("p e c -> p c e"))
         for h in range(2):
-            x_mx[0, h] = (words[:, halves[h]], scales[:, halves[h]])
+            words, scales = quantize("x0%d" % h, x_bf0[h][:].rearrange("p c t -> p (c t)"), HALF)
+            x_mx[0, h] = (words[:], scales[:])
 
         pairs = [keep.tile([P, T, 2], BF16, name="pairs%d" % u, align_bytes=64) for u in range(2)]
 
@@ -97,15 +99,14 @@ def tile_picked_lerp_gelu_e_kernel(tc, xT, w1, frac, offs, left, right, out):
         def pick_pairs(u):
             window = pairs[u][:].rearrange("p t e -> p (t e)").bitcast(U32)
             for h in range(2):
-                picks = offs_sb[:, h * (HALF // 16) : (h + 1) * (HALF // 16)]
-                nc.vector.tensor_copy(got[h][:, u, :], window.indirect(picks))
+                nc.vector.tensor_copy(got[h][:, u, :], window.indirect(lists[h]))
 
-        pair_up(nc.vector.tensor_copy, 0, 0, FIRST_SPLIT)
-        pair_up(nc.scalar.copy, 0, FIRST_SPLIT, T)
-        pick_pairs(0)
+        pair_up(nc.scalar.copy, 0, 0, T // 2)
         pair_up(nc.scalar.copy, 1, 0, T // 2)
-        pair_up(nc.vector.tensor_copy, 2, 0, LAST_SPLIT)
-        pair_up(nc.scalar.copy, 2, LAST_SPLIT, T // 2)
+        pick_pairs(0)
+        pair_up(nc.scalar.copy, 2, 0, T // 2)
+        pair_up(nc.vector.tensor_copy, 3, 0, LAST_SPLIT)
+        pair_up(nc.scalar.copy, 3, LAST_SPLIT, T // 2)
         pick_pairs(1)
         x_bf1 = [keep.tile([P, HALF, 2], I32, name="x_bf1%d" % h, align_bytes=64) for h in range(2)]
         for h in range(2):
@@ -116,8 +117,6 @@ def tile_picked_lerp_gelu_e_kernel(tc, xT, w1, frac, offs, left, right, out):
         for z in range(2):
             interleave(nc.scalar.copy, w_bf_low[z][:], w_raw[z, 0])
             interleave(nc.scalar.copy, w_bf_high[:, z], w_raw[z, 1])
-        rest = keep.tile([P, V], F32, name="rest")
-        nc.scalar.activation(rest[:], frac_sb[:], ACT.Copy, bias=1.0, scale=-1.0)
 
         y = [keep.tile([P, S], F32, name="y%d" % m) for m in range(2)]
         acc = {(m, h): psum.tile([P, HALF], F32, name="acc%d%d" % (m, h)) for m in range(2) for h in range(2)}
@@ -152,6 +151,8 @@ def tile_picked_lerp_gelu_e_kernel(tc, xT, w1, frac, offs, left, right, out):
         w_mx[1, 0] = (words[:], scales[:])
         product(1, 0, 0)
         product(1, 0, 1)
+        rest = keep.tile([P, V], F32, name="rest", tag="w10_words", align_bytes=64)
+        nc.scalar.activation(rest[:], frac_sb[:], ACT.Copy, bias=1.0, scale=-1.0)
 
         words, scales = quantize("w_high", w_bf_high[:].rearrange("p z c t -> p (z c t)"), 2 * P)
         for z in range(2):
@@ -171,18 +172,8 @@ def tile_picked_lerp_gelu_e_kernel(tc, xT, w1, frac, offs, left, right, out):
         nc.vector.tensor_tensor(from_right[0][:], y[0][:].indirect(right_sb[:]), frac_sb[:], ALU.mult)
         nc.vector.tensor_tensor(from_left[0][:], y[0][:].indirect(left_sb[:]), rest[:], ALU.mult)
         nc.vector.tensor_tensor(from_right[1][:], y[1][:].indirect(right_sb[:]), frac_sb[:], ALU.mult)
-        samples = [slice(0, V // 2), slice(V // 2, V)]
-
-        def last_left(part):
-            picks = left_sb[:, part.start // 16 : part.stop // 16]
-            nc.vector.tensor_tensor(from_left[1][:, part], y[1][:].indirect(picks), rest[:, part], ALU.mult)
-
-        last_left(samples[0])
-        result0 = keep.tile([P, V], F32, name="result0", tag="frac_sb")
-        nc.vector.tensor_tensor(result0[:], from_left[0][:], from_right[0][:], ALU.add)
-        nc.sync.dma_start(out[0:P, :], result0[:])
-        last_left(samples[1])
-        result1 = keep.tile([P, V], F32, name="result1")
-        for part in samples:
-            nc.vector.tensor_tensor(result1[:, part], from_left[1][:, part], from_right[1][:, part], ALU.add)
-        nc.sync.dma_start(out[P:N, :], result1[:])
+        nc.vector.tensor_tensor(from_left[1][:], y[1][:].indirect(left_sb[:]), rest[:], ALU.mult)
+        for m, tag in enumerate(("frac_sb", "result1")):
+            result = keep.tile([P, V], F32, name="result%d" % m, tag=tag)
+            nc.vector.tensor_tensor(result[:], from_left[m][:], from_right[m][:], ALU.add)
+            nc.sync.dma_start(out[m * P : (m + 1) * P, :], result[:])

@@ -20,7 +20,8 @@ PACK = 4
 K_PASS = P * PACK
 HALF = S // 2
 PAIR_LOADS = ((0, 0, T // 2), (0, T // 2, T), (1, 0, T // 2), (1, T // 2, T))
-LAST_SPLIT = 264
+LAST_SPLIT = 352
+WORD_SPLIT = 224
 
 
 def interleave(copy, dst, src):
@@ -31,6 +32,7 @@ def tile_picked_lerp_gelu_e_kernel(tc, xT, w1, frac, offs, left, right, out):
     nc = tc.nc
     with ExitStack() as ctx:
         keep = ctx.enter_context(tc.tile_pool(name="keep", bufs=1))
+        shared = ctx.enter_context(tc.tile_pool(name="shared", bufs=1))
         psum = ctx.enter_context(tc.psum_pool(name="psum", bufs=1))
 
         offs_sb = keep.tile([P, S // 16], U16, name="offs_sb")
@@ -55,7 +57,7 @@ def tile_picked_lerp_gelu_e_kernel(tc, xT, w1, frac, offs, left, right, out):
             nc.sync.dma_start(x_part[-1][:], x_rows[1, :, 2 * u : 2 * u + 2, first:last])
         w_raw = {}
         for z in range(2):
-            raw = keep.tile([P, PACK, N], F32, name="w_raw%d" % z, align_bytes=64)
+            raw = shared.tile([P, PACK, N], F32, name="w_raw%d" % z, align_bytes=64, offset=z * PACK * N * 4)
             nc.sync.dma_start(raw[:], w1[z * K_PASS : (z + 1) * K_PASS, :].rearrange("(p j) m -> p j m", j=PACK))
             w_raw[z, 0] = raw[:, :, 0:P]
             w_raw[z, 1] = raw[:, :, P:N]
@@ -66,8 +68,9 @@ def tile_picked_lerp_gelu_e_kernel(tc, xT, w1, frac, offs, left, right, out):
 
         halves = [slice(h * HALF, (h + 1) * HALF) for h in range(2)]
 
-        def quantize(name, grouped, n):
-            words = keep.tile([P, n], U32, name=name + "_words", align_bytes=64)
+        def quantize(name, grouped, n, words=None):
+            if words is None:
+                words = keep.tile([P, n], U32, name=name + "_words", align_bytes=64)
             scales = keep.tile([P, n], U8, name=name + "_scales", align_bytes=64)
             nc.vector.quantize_mx(out=words[:].bitcast(FP8X4), scales=scales[:], in_=grouped)
             return words, scales
@@ -94,7 +97,10 @@ def tile_picked_lerp_gelu_e_kernel(tc, xT, w1, frac, offs, left, right, out):
             u, base = PAIR_LOADS[part][:2]
             copy(pairs[u][:, base + first : base + last, :], x_part[part][:, :, first:last].rearrange("p e t -> p t e"))
 
-        got = [keep.tile([P, 2, HALF], U32, name="got%d" % h, align_bytes=64) for h in range(2)]
+        got = [
+            keep.tile([P, 2, HALF], U32, name="got%d" % h, tag=tag, align_bytes=64)
+            for h, tag in enumerate(("got0", "x_part2"))
+        ]
 
         def pick_pairs(u):
             window = pairs[u][:].rearrange("p t e -> p (t e)").bitcast(U32)
@@ -103,20 +109,28 @@ def tile_picked_lerp_gelu_e_kernel(tc, xT, w1, frac, offs, left, right, out):
 
         pair_up(nc.scalar.copy, 0, 0, T // 2)
         pair_up(nc.scalar.copy, 1, 0, T // 2)
-        pick_pairs(0)
         pair_up(nc.scalar.copy, 2, 0, T // 2)
+        pick_pairs(0)
         pair_up(nc.vector.tensor_copy, 3, 0, LAST_SPLIT)
         pair_up(nc.scalar.copy, 3, LAST_SPLIT, T // 2)
         pick_pairs(1)
-        x_bf1 = [keep.tile([P, HALF, 2], I32, name="x_bf1%d" % h, align_bytes=64) for h in range(2)]
-        for h in range(2):
-            nc.vector.tensor_copy(x_bf1[h][:], got[h][:].bitcast(I32).rearrange("p u c -> p c u"))
+        x_bf1 = [
+            keep.tile([P, HALF, 2], U32, name="x_bf10", align_bytes=64),
+            shared.tile([P, HALF, 2], U32, name="x_bf11", align_bytes=64, offset=HALF * 4),
+        ]
+        for h, width in enumerate((HALF, WORD_SPLIT)):
+            nc.vector.tensor_copy(
+                x_bf1[h][:].bitcast(I32)[:, :width, :],
+                got[h][:].bitcast(I32)[:, :, :width].rearrange("p u c -> p c u"),
+            )
 
         w_bf_low = [keep.tile([P, P, PACK], BF16, name="w_bf_low%d" % z, align_bytes=64) for z in range(2)]
         w_bf_high = keep.tile([P, 2, P, PACK], BF16, name="w_bf_high", align_bytes=64)
-        for z in range(2):
-            interleave(nc.scalar.copy, w_bf_low[z][:], w_raw[z, 0])
-            interleave(nc.scalar.copy, w_bf_high[:, z], w_raw[z, 1])
+        interleave(nc.scalar.copy, w_bf_low[0][:], w_raw[0, 0])
+        interleave(nc.scalar.copy, w_bf_low[1][:], w_raw[1, 0])
+        interleave(nc.scalar.copy, w_bf_high[:, 0], w_raw[0, 1])
+        nc.scalar.copy(x_bf1[1][:, WORD_SPLIT:, :], got[1][:, :, WORD_SPLIT:].rearrange("p u c -> p c u"))
+        interleave(nc.scalar.copy, w_bf_high[:, 1], w_raw[1, 1])
 
         y = [keep.tile([P, S], F32, name="y%d" % m) for m in range(2)]
         acc = {(m, h): psum.tile([P, HALF], F32, name="acc%d%d" % (m, h)) for m in range(2) for h in range(2)}
@@ -138,18 +152,14 @@ def tile_picked_lerp_gelu_e_kernel(tc, xT, w1, frac, offs, left, right, out):
         w_mx[0, 0] = (words[:], scales[:])
         product(0, 0, 0)
         product(0, 0, 1)
-        x1_words = keep.tile([P, S], U32, name="x1_words", tag="w_raw0", align_bytes=64)
-        x1_scales = keep.tile([P, S], U8, name="x1_scales", align_bytes=64)
-        for h in range(2):
-            x_mx[1, h] = (x1_words[:, halves[h]], x1_scales[:, halves[h]])
-            nc.vector.quantize_mx(
-                out=x_mx[1, h][0].bitcast(FP8X4),
-                scales=x_mx[1, h][1],
-                in_=x_bf1[h][:].rearrange("p c u -> p (c u)").bitcast(BF16),
-            )
+        words = shared.tile([P, HALF], U32, name="x10_words", align_bytes=64, offset=0)
+        words, scales = quantize("x10", x_bf1[0][:].rearrange("p c u -> p (c u)").bitcast(BF16), HALF, words)
+        x_mx[1, 0] = (words[:], scales[:])
         words, scales = quantize("w10", w_bf_low[1][:].rearrange("p c t -> p (c t)"), P)
         w_mx[1, 0] = (words[:], scales[:])
         product(1, 0, 0)
+        words, scales = quantize("x11", x_bf1[1][:].rearrange("p c u -> p (c u)").bitcast(BF16), HALF)
+        x_mx[1, 1] = (words[:], scales[:])
         product(1, 0, 1)
         rest = keep.tile([P, V], F32, name="rest", tag="w10_words", align_bytes=64)
         nc.scalar.activation(rest[:], frac_sb[:], ACT.Copy, bias=1.0, scale=-1.0)

@@ -19,9 +19,9 @@ P = 128
 PACK = 4
 K_PASS = P * PACK
 HALF = S // 2
-PAIR_LOADS = ((0, 0, T // 2), (0, T // 2, T), (1, 0, T // 2), (1, T // 2, T))
-LAST_SPLIT = 352
-WORD_SPLIT = 224
+EARLY_SPLIT = 672
+LAST_SPLIT = 320
+W_SPLIT = 48
 
 
 def interleave(copy, dst, src):
@@ -44,17 +44,17 @@ def tile_picked_lerp_gelu_e_kernel(tc, xT, w1, frac, offs, left, right, out):
         nc.vector.memset(warm[:], 0.0)
         nc.scalar.activation(warm_out[:], warm[:], ACT.Gelu_apprx_tanh)
 
-        x_rows = xT.rearrange("(z p j) t -> z p j t", p=P, j=PACK)
-        x_plane = []
-        for j in range(PACK):
-            x_plane.append(keep.tile([P, T], F32, name="x_plane%d" % j, align_bytes=64))
-            nc.sync.dma_start(x_plane[j][:], x_rows[0, :, j, :])
-            if j == 0:
-                nc.sync.dma_start(offs_sb[:], offs)
-        x_part = []
-        for u, first, last in PAIR_LOADS:
-            x_part.append(keep.tile([P, 2, last - first], F32, name="x_part%d" % len(x_part), align_bytes=64))
-            nc.sync.dma_start(x_part[-1][:], x_rows[1, :, 2 * u : 2 * u + 2, first:last])
+        x_rows = xT.rearrange("(z p u e) t -> z u p e t", p=P, u=2, e=2)
+        raw00 = keep.tile([P, 2, T], F32, name="raw00", align_bytes=64)
+        nc.sync.dma_start(raw00[:], x_rows[0, 0])
+        nc.sync.dma_start(offs_sb[:], offs)
+        raw01 = keep.tile([P, 2, T], F32, name="raw01", align_bytes=64)
+        nc.sync.dma_start(raw01[:], x_rows[0, 1])
+        raw10, raw11 = [], []
+        for u, parts in enumerate((raw10, raw11)):
+            for part in range(2):
+                parts.append(keep.tile([P, 2, T // 2], F32, name="raw1%d%d" % (u, part), align_bytes=64))
+                nc.sync.dma_start(parts[part][:], x_rows[1, u, :, :, part * (T // 2) : (part + 1) * (T // 2)])
         w_raw = {}
         for z in range(2):
             raw = shared.tile([P, PACK, N], F32, name="w_raw%d" % z, align_bytes=64, offset=z * PACK * N * 4)
@@ -67,6 +67,7 @@ def tile_picked_lerp_gelu_e_kernel(tc, xT, w1, frac, offs, left, right, out):
         nc.sync.dma_start(left_sb[:], left)
 
         halves = [slice(h * HALF, (h + 1) * HALF) for h in range(2)]
+        lists = [offs_sb[:, h * (HALF // 16) : (h + 1) * (HALF // 16)] for h in range(2)]
 
         def quantize(name, grouped, n, words=None):
             if words is None:
@@ -77,59 +78,64 @@ def tile_picked_lerp_gelu_e_kernel(tc, xT, w1, frac, offs, left, right, out):
 
         x_mx = {}
         w_mx = {}
+        pairs = {
+            (z, u): keep.tile([P, T, 2], BF16, name="pairs%d%d" % (z, u), align_bytes=64)
+            for z in range(2)
+            for u in range(2)
+        }
+        got = [keep.tile([P, 2, 2, HALF], U32, name="got%d" % z, align_bytes=64) for z in range(2)]
 
-        lists = [offs_sb[:, h * (HALF // 16) : (h + 1) * (HALF // 16)] for h in range(2)]
-        picked = [keep.tile([P, 2, S], F32, name="picked%d" % u) for u in range(2)]
-        x_bf0 = [keep.tile([P, HALF, PACK], BF16, name="x_bf0%d" % h, align_bytes=64) for h in range(2)]
-        for u, copy in enumerate((nc.scalar.copy, nc.vector.tensor_copy)):
-            nc.vector.tensor_copy(picked[u][:, 0, :], x_plane[2 * u][:].indirect(offs_sb[:]))
+        def pair_up(copy, z, u, raw, first, last, base=0):
+            copy(pairs[z, u][:, base + first : base + last, :], raw[:, :, first:last].rearrange("p e t -> p t e"))
+
+        def window(z, u):
+            return pairs[z, u][:].rearrange("p t e -> p (t e)").bitcast(U32)
+
+        def pick_whole(z):
+            nc.vector.tensor_copy(got[z][:, :, 0, :], window(z, 0).indirect(offs_sb[:]))
+
+        def pick_halves(z):
             for h in range(2):
-                nc.vector.tensor_copy(picked[u][:, 1, halves[h]], x_plane[2 * u + 1][:].indirect(lists[h]))
-            for h in range(2):
-                copy(x_bf0[h][:, :, 2 * u : 2 * u + 2], picked[u][:, :, halves[h]].rearrange("p e c -> p c e"))
-        for h in range(2):
-            words, scales = quantize("x0%d" % h, x_bf0[h][:].rearrange("p c t -> p (c t)"), HALF)
-            x_mx[0, h] = (words[:], scales[:])
+                nc.vector.tensor_copy(got[z][:, h, 1, :], window(z, 1).indirect(lists[h]))
 
-        pairs = [keep.tile([P, T, 2], BF16, name="pairs%d" % u, align_bytes=64) for u in range(2)]
-
-        def pair_up(copy, part, first, last):
-            u, base = PAIR_LOADS[part][:2]
-            copy(pairs[u][:, base + first : base + last, :], x_part[part][:, :, first:last].rearrange("p e t -> p t e"))
-
-        got = [
-            keep.tile([P, 2, HALF], U32, name="got%d" % h, tag=tag, align_bytes=64)
-            for h, tag in enumerate(("got0", "x_part2"))
-        ]
-
-        def pick_pairs(u):
-            window = pairs[u][:].rearrange("p t e -> p (t e)").bitcast(U32)
-            for h in range(2):
-                nc.vector.tensor_copy(got[h][:, u, :], window.indirect(lists[h]))
-
-        pair_up(nc.scalar.copy, 0, 0, T // 2)
-        pair_up(nc.scalar.copy, 1, 0, T // 2)
-        pair_up(nc.scalar.copy, 2, 0, T // 2)
-        pick_pairs(0)
-        pair_up(nc.vector.tensor_copy, 3, 0, LAST_SPLIT)
-        pair_up(nc.scalar.copy, 3, LAST_SPLIT, T // 2)
-        pick_pairs(1)
-        x_bf1 = [
-            keep.tile([P, HALF, 2], U32, name="x_bf10", align_bytes=64),
-            shared.tile([P, HALF, 2], U32, name="x_bf11", align_bytes=64, offset=HALF * 4),
-        ]
-        for h, width in enumerate((HALF, WORD_SPLIT)):
+        def weave(z, h, dst):
             nc.vector.tensor_copy(
-                x_bf1[h][:].bitcast(I32)[:, :width, :],
-                got[h][:].bitcast(I32)[:, :, :width].rearrange("p u c -> p c u"),
+                dst.bitcast(I32).rearrange("p (c u) -> p c u", u=2),
+                got[z][:, h].bitcast(I32).rearrange("p u c -> p c u"),
             )
+
+        for u, raw in enumerate((raw00, raw01)):
+            pair_up(nc.vector.tensor_copy, 0, u, raw[:], 0, EARLY_SPLIT)
+            pair_up(nc.scalar.copy, 0, u, raw[:], EARLY_SPLIT, T)
+            if u == 0:
+                pick_whole(0)
+        pick_halves(0)
+
+        x_bf0 = [keep.tile([P, S], F32, name="x_bf0%d" % h, align_bytes=64)[:] for h in range(2)]
+        for h in range(2):
+            weave(0, h, x_bf0[h])
+        for part in range(2):
+            pair_up(nc.scalar.copy, 1, 0, raw10[part][:], 0, T // 2, part * (T // 2))
+        words, scales = quantize("x00", x_bf0[0].bitcast(BF16), HALF)
+        x_mx[0, 0] = (words[:], scales[:])
+        pick_whole(1)
+
+        pair_up(nc.scalar.copy, 1, 1, raw11[0][:], 0, T // 2)
+        pair_up(nc.vector.tensor_copy, 1, 1, raw11[1][:], 0, LAST_SPLIT, T // 2)
+        pair_up(nc.scalar.copy, 1, 1, raw11[1][:], LAST_SPLIT, T // 2, T // 2)
+        words = keep.tile([P, HALF], U32, name="x01_words", tag="raw110", align_bytes=64)
+        words, scales = quantize("x01", x_bf0[1].bitcast(BF16), HALF, words)
+        x_mx[0, 1] = (words[:], scales[:])
+        pick_halves(1)
+        x_bf1 = [keep.tile([P, S], F32, name="x_bf1%d" % h, align_bytes=64) for h in range(2)]
+        for h in range(2):
+            weave(1, h, x_bf1[h][:])
 
         w_bf_low = [keep.tile([P, P, PACK], BF16, name="w_bf_low%d" % z, align_bytes=64) for z in range(2)]
         w_bf_high = keep.tile([P, 2, P, PACK], BF16, name="w_bf_high", align_bytes=64)
         interleave(nc.scalar.copy, w_bf_low[0][:], w_raw[0, 0])
-        interleave(nc.scalar.copy, w_bf_low[1][:], w_raw[1, 0])
         interleave(nc.scalar.copy, w_bf_high[:, 0], w_raw[0, 1])
-        nc.scalar.copy(x_bf1[1][:, WORD_SPLIT:, :], got[1][:, :, WORD_SPLIT:].rearrange("p u c -> p c u"))
+        interleave(nc.scalar.copy, w_bf_low[1][:, :W_SPLIT], w_raw[1, 0][:, :, :W_SPLIT])
         interleave(nc.scalar.copy, w_bf_high[:, 1], w_raw[1, 1])
 
         y = [keep.tile([P, S], F32, name="y%d" % m) for m in range(2)]
@@ -152,14 +158,18 @@ def tile_picked_lerp_gelu_e_kernel(tc, xT, w1, frac, offs, left, right, out):
         w_mx[0, 0] = (words[:], scales[:])
         product(0, 0, 0)
         product(0, 0, 1)
-        words = shared.tile([P, HALF], U32, name="x10_words", align_bytes=64, offset=0)
-        words, scales = quantize("x10", x_bf1[0][:].rearrange("p c u -> p (c u)").bitcast(BF16), HALF, words)
-        x_mx[1, 0] = (words[:], scales[:])
+        interleave(nc.vector.tensor_copy, w_bf_low[1][:, W_SPLIT:], w_raw[1, 0][:, :, W_SPLIT:])
+
+        def quantize_x1(h):
+            words = shared.tile([P, HALF], U32, name="x1%d_words" % h, align_bytes=64, offset=h * HALF * 4)
+            words, scales = quantize("x1%d" % h, x_bf1[h][:].bitcast(BF16), HALF, words)
+            x_mx[1, h] = (words[:], scales[:])
+
+        quantize_x1(0)
         words, scales = quantize("w10", w_bf_low[1][:].rearrange("p c t -> p (c t)"), P)
         w_mx[1, 0] = (words[:], scales[:])
         product(1, 0, 0)
-        words, scales = quantize("x11", x_bf1[1][:].rearrange("p c u -> p (c u)").bitcast(BF16), HALF)
-        x_mx[1, 1] = (words[:], scales[:])
+        quantize_x1(1)
         product(1, 0, 1)
         rest = keep.tile([P, V], F32, name="rest", tag="w10_words", align_bytes=64)
         nc.scalar.activation(rest[:], frac_sb[:], ACT.Copy, bias=1.0, scale=-1.0)
@@ -167,22 +177,15 @@ def tile_picked_lerp_gelu_e_kernel(tc, xT, w1, frac, offs, left, right, out):
         words, scales = quantize("w_high", w_bf_high[:].rearrange("p z c t -> p (z c t)"), 2 * P)
         for z in range(2):
             w_mx[z, 1] = (words[:, z * P : (z + 1) * P], scales[:, z * P : (z + 1) * P])
-        for z in range(2):
-            for h in range(2):
+        for h in range(2):
+            for z in range(2):
                 product(z, 1, h)
 
-        from_right = [
-            keep.tile([P, V], F32, name="from_right0"),
-            keep.tile([P, V], F32, name="from_right1"),
-        ]
-        from_left = [
-            keep.tile([P, V], F32, name="from_left0"),
-            keep.tile([P, V], F32, name="from_left1"),
-        ]
-        nc.vector.tensor_tensor(from_right[0][:], y[0][:].indirect(right_sb[:]), frac_sb[:], ALU.mult)
-        nc.vector.tensor_tensor(from_left[0][:], y[0][:].indirect(left_sb[:]), rest[:], ALU.mult)
-        nc.vector.tensor_tensor(from_right[1][:], y[1][:].indirect(right_sb[:]), frac_sb[:], ALU.mult)
-        nc.vector.tensor_tensor(from_left[1][:], y[1][:].indirect(left_sb[:]), rest[:], ALU.mult)
+        from_right = [keep.tile([P, V], F32, name="from_right%d" % m) for m in range(2)]
+        from_left = [keep.tile([P, V], F32, name="from_left%d" % m) for m in range(2)]
+        for m in range(2):
+            nc.vector.tensor_tensor(from_right[m][:], y[m][:].indirect(right_sb[:]), frac_sb[:], ALU.mult)
+            nc.vector.tensor_tensor(from_left[m][:], y[m][:].indirect(left_sb[:]), rest[:], ALU.mult)
         for m, tag in enumerate(("frac_sb", "result1")):
             result = keep.tile([P, V], F32, name="result%d" % m, tag=tag)
             nc.vector.tensor_tensor(result[:], from_left[m][:], from_right[m][:], ALU.add)

@@ -20,8 +20,9 @@ PACK = 4
 K_PASS = P * PACK
 HALF = S // 2
 EARLY_SPLIT = 672
+MID_SPLIT = 256
 LAST_SPLIT = 320
-W_SPLIT = 48
+WORD_SPLIT = 224
 
 
 def interleave(copy, dst, src):
@@ -48,13 +49,11 @@ def tile_picked_lerp_gelu_e_kernel(tc, xT, w1, frac, offs, left, right, out):
         raw00 = keep.tile([P, 2, T], F32, name="raw00", align_bytes=64)
         nc.sync.dma_start(raw00[:], x_rows[0, 0])
         nc.sync.dma_start(offs_sb[:], offs)
-        raw01 = keep.tile([P, 2, T], F32, name="raw01", align_bytes=64)
-        nc.sync.dma_start(raw01[:], x_rows[0, 1])
-        raw10, raw11 = [], []
-        for u, parts in enumerate((raw10, raw11)):
+        raw01, raw10, raw11 = [], [], []
+        for (z, u), parts in (((0, 1), raw01), ((1, 0), raw10), ((1, 1), raw11)):
             for part in range(2):
-                parts.append(keep.tile([P, 2, T // 2], F32, name="raw1%d%d" % (u, part), align_bytes=64))
-                nc.sync.dma_start(parts[part][:], x_rows[1, u, :, :, part * (T // 2) : (part + 1) * (T // 2)])
+                parts.append(keep.tile([P, 2, T // 2], F32, name="raw%d%d%d" % (z, u, part), align_bytes=64))
+                nc.sync.dma_start(parts[part][:], x_rows[z, u, :, :, part * (T // 2) : (part + 1) * (T // 2)])
         w_raw = {}
         for z in range(2):
             raw = shared.tile([P, PACK, N], F32, name="w_raw%d" % z, align_bytes=64, offset=z * PACK * N * 4)
@@ -98,44 +97,53 @@ def tile_picked_lerp_gelu_e_kernel(tc, xT, w1, frac, offs, left, right, out):
             for h in range(2):
                 nc.vector.tensor_copy(got[z][:, h, 1, :], window(z, 1).indirect(lists[h]))
 
-        def weave(z, h, dst):
+        def weave(z, h, dst, width=HALF):
             nc.vector.tensor_copy(
-                dst.bitcast(I32).rearrange("p (c u) -> p c u", u=2),
-                got[z][:, h].bitcast(I32).rearrange("p u c -> p c u"),
+                dst.bitcast(I32).rearrange("p (c u) -> p c u", u=2)[:, :width, :],
+                got[z][:, h].bitcast(I32)[:, :, :width].rearrange("p u c -> p c u"),
             )
 
-        for u, raw in enumerate((raw00, raw01)):
-            pair_up(nc.vector.tensor_copy, 0, u, raw[:], 0, EARLY_SPLIT)
-            pair_up(nc.scalar.copy, 0, u, raw[:], EARLY_SPLIT, T)
-            if u == 0:
-                pick_whole(0)
+        def pair_up_parts(z, u, parts, split):
+            pair_up(nc.scalar.copy, z, u, parts[0][:], 0, T // 2)
+            pair_up(nc.vector.tensor_copy, z, u, parts[1][:], 0, split, T // 2)
+            pair_up(nc.scalar.copy, z, u, parts[1][:], split, T // 2, T // 2)
+
+        pair_up(nc.vector.tensor_copy, 0, 0, raw00[:], 0, EARLY_SPLIT)
+        pair_up(nc.scalar.copy, 0, 0, raw00[:], EARLY_SPLIT, T)
+        pick_whole(0)
+        pair_up_parts(0, 1, raw01, LAST_SPLIT)
         pick_halves(0)
 
         x_bf0 = [keep.tile([P, S], F32, name="x_bf0%d" % h, align_bytes=64)[:] for h in range(2)]
         for h in range(2):
             weave(0, h, x_bf0[h])
-        for part in range(2):
-            pair_up(nc.scalar.copy, 1, 0, raw10[part][:], 0, T // 2, part * (T // 2))
-        words, scales = quantize("x00", x_bf0[0].bitcast(BF16), HALF)
+        pair_up_parts(1, 0, raw10, MID_SPLIT)
+        words = keep.tile([P, HALF], U32, name="x00_words", tag="raw100", align_bytes=64)
+        words, scales = quantize("x00", x_bf0[0].bitcast(BF16), HALF, words)
         x_mx[0, 0] = (words[:], scales[:])
         pick_whole(1)
 
-        pair_up(nc.scalar.copy, 1, 1, raw11[0][:], 0, T // 2)
-        pair_up(nc.vector.tensor_copy, 1, 1, raw11[1][:], 0, LAST_SPLIT, T // 2)
-        pair_up(nc.scalar.copy, 1, 1, raw11[1][:], LAST_SPLIT, T // 2, T // 2)
+        pair_up_parts(1, 1, raw11, LAST_SPLIT)
         words = keep.tile([P, HALF], U32, name="x01_words", tag="raw110", align_bytes=64)
         words, scales = quantize("x01", x_bf0[1].bitcast(BF16), HALF, words)
         x_mx[0, 1] = (words[:], scales[:])
         pick_halves(1)
-        x_bf1 = [keep.tile([P, S], F32, name="x_bf1%d" % h, align_bytes=64) for h in range(2)]
-        for h in range(2):
-            weave(1, h, x_bf1[h][:])
+        x_bf1 = [
+            keep.tile([P, S], U32, name="x_bf10", align_bytes=64),
+            shared.tile([P, S], U32, name="x_bf11", align_bytes=64, offset=HALF * 4),
+        ]
+        for h, width in enumerate((HALF, WORD_SPLIT)):
+            weave(1, h, x_bf1[h][:], width)
 
         w_bf_low = [keep.tile([P, P, PACK], BF16, name="w_bf_low%d" % z, align_bytes=64) for z in range(2)]
         w_bf_high = keep.tile([P, 2, P, PACK], BF16, name="w_bf_high", align_bytes=64)
         interleave(nc.scalar.copy, w_bf_low[0][:], w_raw[0, 0])
+        interleave(nc.scalar.copy, w_bf_low[1][:], w_raw[1, 0])
         interleave(nc.scalar.copy, w_bf_high[:, 0], w_raw[0, 1])
-        interleave(nc.scalar.copy, w_bf_low[1][:, :W_SPLIT], w_raw[1, 0][:, :, :W_SPLIT])
+        nc.scalar.copy(
+            x_bf1[1][:].rearrange("p (c u) -> p c u", u=2)[:, WORD_SPLIT:, :],
+            got[1][:, 1, :, WORD_SPLIT:].rearrange("p u c -> p c u"),
+        )
         interleave(nc.scalar.copy, w_bf_high[:, 1], w_raw[1, 1])
 
         y = [keep.tile([P, S], F32, name="y%d" % m) for m in range(2)]
@@ -158,10 +166,9 @@ def tile_picked_lerp_gelu_e_kernel(tc, xT, w1, frac, offs, left, right, out):
         w_mx[0, 0] = (words[:], scales[:])
         product(0, 0, 0)
         product(0, 0, 1)
-        interleave(nc.vector.tensor_copy, w_bf_low[1][:, W_SPLIT:], w_raw[1, 0][:, :, W_SPLIT:])
 
         def quantize_x1(h):
-            words = shared.tile([P, HALF], U32, name="x1%d_words" % h, align_bytes=64, offset=h * HALF * 4)
+            words = shared.tile([P, HALF], U32, name="x10_words", align_bytes=64, offset=0) if h == 0 else None
             words, scales = quantize("x1%d" % h, x_bf1[h][:].bitcast(BF16), HALF, words)
             x_mx[1, h] = (words[:], scales[:])
 
@@ -177,8 +184,8 @@ def tile_picked_lerp_gelu_e_kernel(tc, xT, w1, frac, offs, left, right, out):
         words, scales = quantize("w_high", w_bf_high[:].rearrange("p z c t -> p (z c t)"), 2 * P)
         for z in range(2):
             w_mx[z, 1] = (words[:, z * P : (z + 1) * P], scales[:, z * P : (z + 1) * P])
-        for h in range(2):
-            for z in range(2):
+        for z in range(2):
+            for h in range(2):
                 product(z, 1, h)
 
         from_right = [keep.tile([P, V], F32, name="from_right%d" % m) for m in range(2)]

@@ -20,7 +20,7 @@ PACK = 4
 K_PASS = P * PACK
 HALF = S // 2
 EARLY_SPLIT = 672
-MID_SPLIT = 256
+MID_SPLIT = 128
 LAST_SPLIT = 320
 WORD_SPLIT = 224
 
@@ -49,11 +49,13 @@ def tile_picked_lerp_gelu_e_kernel(tc, xT, w1, frac, offs, left, right, out):
         raw00 = keep.tile([P, 2, T], F32, name="raw00", align_bytes=64)
         nc.sync.dma_start(raw00[:], x_rows[0, 0])
         nc.sync.dma_start(offs_sb[:], offs)
-        raw01, raw10, raw11 = [], [], []
-        for (z, u), parts in (((0, 1), raw01), ((1, 0), raw10), ((1, 1), raw11)):
+        raw01 = keep.tile([P, 2, T], F32, name="raw01", align_bytes=64)
+        nc.sync.dma_start(raw01[:], x_rows[0, 1])
+        raw10, raw11 = [], []
+        for u, parts in enumerate((raw10, raw11)):
             for part in range(2):
-                parts.append(keep.tile([P, 2, T // 2], F32, name="raw%d%d%d" % (z, u, part), align_bytes=64))
-                nc.sync.dma_start(parts[part][:], x_rows[z, u, :, :, part * (T // 2) : (part + 1) * (T // 2)])
+                parts.append(keep.tile([P, 2, T // 2], F32, name="raw1%d%d" % (u, part), align_bytes=64))
+                nc.sync.dma_start(parts[part][:], x_rows[1, u, :, :, part * (T // 2) : (part + 1) * (T // 2)])
         w_raw = {}
         for z in range(2):
             raw = shared.tile([P, PACK, N], F32, name="w_raw%d" % z, align_bytes=64, offset=z * PACK * N * 4)
@@ -108,10 +110,11 @@ def tile_picked_lerp_gelu_e_kernel(tc, xT, w1, frac, offs, left, right, out):
             pair_up(nc.vector.tensor_copy, z, u, parts[1][:], 0, split, T // 2)
             pair_up(nc.scalar.copy, z, u, parts[1][:], split, T // 2, T // 2)
 
-        pair_up(nc.vector.tensor_copy, 0, 0, raw00[:], 0, EARLY_SPLIT)
-        pair_up(nc.scalar.copy, 0, 0, raw00[:], EARLY_SPLIT, T)
-        pick_whole(0)
-        pair_up_parts(0, 1, raw01, LAST_SPLIT)
+        for u, raw in enumerate((raw00, raw01)):
+            pair_up(nc.vector.tensor_copy, 0, u, raw[:], 0, EARLY_SPLIT)
+            pair_up(nc.scalar.copy, 0, u, raw[:], EARLY_SPLIT, T)
+            if u == 0:
+                pick_whole(0)
         pick_halves(0)
 
         x_bf0 = [keep.tile([P, S], F32, name="x_bf0%d" % h, align_bytes=64)[:] for h in range(2)]

@@ -8,7 +8,6 @@ FLOPS = 2 * K * S * N
 F32 = mybir.dt.float32
 BF16 = mybir.dt.bfloat16
 U32 = mybir.dt.uint32
-I32 = mybir.dt.int32
 U16 = mybir.dt.uint16
 U8 = mybir.dt.uint8
 FP8X4 = mybir.dt.float8_e4m3fn_x4
@@ -19,10 +18,8 @@ P = 128
 PACK = 4
 K_PASS = P * PACK
 HALF = S // 2
-EARLY_SPLIT = 672
-MID_SPLIT = 128
-LAST_SPLIT = 320
-WORD_SPLIT = 224
+SCALAR_FRAMES = 96
+VECTOR_PICKS = 320
 
 
 def interleave(copy, dst, src):
@@ -33,7 +30,6 @@ def tile_picked_lerp_gelu_e_kernel(tc, xT, w1, frac, offs, left, right, out):
     nc = tc.nc
     with ExitStack() as ctx:
         keep = ctx.enter_context(tc.tile_pool(name="keep", bufs=1))
-        shared = ctx.enter_context(tc.tile_pool(name="shared", bufs=1))
         psum = ctx.enter_context(tc.psum_pool(name="psum", bufs=1))
 
         offs_sb = keep.tile([P, S // 16], U16, name="offs_sb")
@@ -45,158 +41,129 @@ def tile_picked_lerp_gelu_e_kernel(tc, xT, w1, frac, offs, left, right, out):
         nc.vector.memset(warm[:], 0.0)
         nc.scalar.activation(warm_out[:], warm[:], ACT.Gelu_apprx_tanh)
 
-        x_rows = xT.rearrange("(z p u e) t -> z u p e t", p=P, u=2, e=2)
-        raw00 = keep.tile([P, 2, T], F32, name="raw00", align_bytes=64)
-        nc.sync.dma_start(raw00[:], x_rows[0, 0])
+        x_rows = xT.rearrange("(z p j) t -> z p j t", p=P, j=PACK)
+        plane = {}
+
+        def load_planes(z, first, count):
+            raw = keep.tile([P, count, T], F32, name="raw%d%d" % (z, first), align_bytes=64)
+            nc.sync.dma_start(raw[:], x_rows[z, :, first : first + count, :])
+            for j in range(count):
+                plane[z, first + j] = raw[:, j, :]
+
+        load_planes(0, 0, 2)
         nc.sync.dma_start(offs_sb[:], offs)
-        raw01 = keep.tile([P, 2, T], F32, name="raw01", align_bytes=64)
-        nc.sync.dma_start(raw01[:], x_rows[0, 1])
-        raw10, raw11 = [], []
-        for u, parts in enumerate((raw10, raw11)):
-            for part in range(2):
-                parts.append(keep.tile([P, 2, T // 2], F32, name="raw1%d%d" % (u, part), align_bytes=64))
-                nc.sync.dma_start(parts[part][:], x_rows[1, u, :, :, part * (T // 2) : (part + 1) * (T // 2)])
-        w_raw = {}
+        for z, j in ((0, 2), (0, 3), (1, 0), (1, 1), (1, 2), (1, 3)):
+            load_planes(z, j, 1)
+        w_raw = []
         for z in range(2):
-            raw = shared.tile([P, PACK, N], F32, name="w_raw%d" % z, align_bytes=64, offset=z * PACK * N * 4)
-            nc.sync.dma_start(raw[:], w1[z * K_PASS : (z + 1) * K_PASS, :].rearrange("(p j) m -> p j m", j=PACK))
-            w_raw[z, 0] = raw[:, :, 0:P]
-            w_raw[z, 1] = raw[:, :, P:N]
+            w_raw.append(keep.tile([P, PACK, N], F32, name="w_raw%d" % z, align_bytes=64))
+            nc.sync.dma_start(w_raw[z][:], w1[z * K_PASS : (z + 1) * K_PASS, :].rearrange("(p j) m -> p j m", j=PACK))
         frac_sb = keep.tile([P, V], F32, name="frac_sb")
         nc.sync.dma_start(frac_sb[:], frac)
         nc.sync.dma_start(right_sb[:], right)
         nc.sync.dma_start(left_sb[:], left)
 
         halves = [slice(h * HALF, (h + 1) * HALF) for h in range(2)]
-        lists = [offs_sb[:, h * (HALF // 16) : (h + 1) * (HALF // 16)] for h in range(2)]
+        picked = [keep.tile([P, PACK, S], F32, name="picked%d" % z, align_bytes=64) for z in range(2)]
 
-        def quantize(name, grouped, n, words=None):
-            if words is None:
-                words = keep.tile([P, n], U32, name=name + "_words", align_bytes=64)
+        def scalar_gather(dst, src):
+            nc.scalar.activation(dst, src, ACT.Copy)
+
+        def pick(copy, z, j, first, last):
+            copy(picked[z][:, j, first:last], plane[z, j].indirect(offs_sb[:, first // 16 : last // 16]))
+
+        def quantize(name, grouped, n):
+            words = keep.tile([P, n], U32, name=name + "_words", align_bytes=64)
             scales = keep.tile([P, n], U8, name=name + "_scales", align_bytes=64)
-            nc.vector.quantize_mx(out=words[:].bitcast(FP8X4), scales=scales[:], in_=grouped)
-            return words, scales
+            nc.vector.quantize_mx(
+                out=words[:].bitcast(FP8X4), scales=scales[:], in_=grouped.rearrange("p c t -> p (c t)")
+            )
+            return words[:], scales[:]
 
+        x_bf = {
+            (z, h): keep.tile([P, HALF, PACK], BF16, name="x_bf%d%d" % (z, h), align_bytes=64)
+            for z in range(2)
+            for h in range(2)
+        }
         x_mx = {}
         w_mx = {}
-        pairs = {
-            (z, u): keep.tile([P, T, 2], BF16, name="pairs%d%d" % (z, u), align_bytes=64)
-            for z in range(2)
-            for u in range(2)
-        }
-        got = [keep.tile([P, 2, 2, HALF], U32, name="got%d" % z, align_bytes=64) for z in range(2)]
 
-        def pair_up(copy, z, u, raw, first, last, base=0):
-            copy(pairs[z, u][:, base + first : base + last, :], raw[:, :, first:last].rearrange("p e t -> p t e"))
-
-        def window(z, u):
-            return pairs[z, u][:].rearrange("p t e -> p (t e)").bitcast(U32)
-
-        def pick_whole(z):
-            nc.vector.tensor_copy(got[z][:, :, 0, :], window(z, 0).indirect(offs_sb[:]))
-
-        def pick_halves(z):
-            for h in range(2):
-                nc.vector.tensor_copy(got[z][:, h, 1, :], window(z, 1).indirect(lists[h]))
-
-        def weave(z, h, dst, width=HALF):
-            nc.vector.tensor_copy(
-                dst.bitcast(I32).rearrange("p (c u) -> p c u", u=2)[:, :width, :],
-                got[z][:, h].bitcast(I32)[:, :, :width].rearrange("p u c -> p c u"),
-            )
-
-        def pair_up_parts(z, u, parts, split):
-            pair_up(nc.scalar.copy, z, u, parts[0][:], 0, T // 2)
-            pair_up(nc.vector.tensor_copy, z, u, parts[1][:], 0, split, T // 2)
-            pair_up(nc.scalar.copy, z, u, parts[1][:], split, T // 2, T // 2)
-
-        for u, raw in enumerate((raw00, raw01)):
-            pair_up(nc.vector.tensor_copy, 0, u, raw[:], 0, EARLY_SPLIT)
-            pair_up(nc.scalar.copy, 0, u, raw[:], EARLY_SPLIT, T)
-            if u == 0:
-                pick_whole(0)
-        pick_halves(0)
-
-        x_bf0 = [keep.tile([P, S], F32, name="x_bf0%d" % h, align_bytes=64)[:] for h in range(2)]
+        pick(scalar_gather, 0, 0, 0, S)
+        pick(nc.vector.tensor_copy, 0, 1, 0, S)
+        pick(scalar_gather, 0, 2, 0, S)
+        pick(nc.vector.tensor_copy, 0, 3, 0, HALF)
+        pick(scalar_gather, 0, 3, HALF, S)
         for h in range(2):
-            weave(0, h, x_bf0[h])
-        pair_up_parts(1, 0, raw10, MID_SPLIT)
-        words = keep.tile([P, HALF], U32, name="x00_words", tag="raw100", align_bytes=64)
-        words, scales = quantize("x00", x_bf0[0].bitcast(BF16), HALF, words)
-        x_mx[0, 0] = (words[:], scales[:])
-        pick_whole(1)
+            interleave(nc.vector.tensor_copy, x_bf[0, h][:], picked[0][:, :, halves[h]])
+        for h in range(2):
+            x_mx[0, h] = quantize("x0%d" % h, x_bf[0, h][:], HALF)
 
-        pair_up_parts(1, 1, raw11, LAST_SPLIT)
-        words = keep.tile([P, HALF], U32, name="x01_words", tag="raw110", align_bytes=64)
-        words, scales = quantize("x01", x_bf0[1].bitcast(BF16), HALF, words)
-        x_mx[0, 1] = (words[:], scales[:])
-        pick_halves(1)
-        x_bf1 = [
-            keep.tile([P, S], U32, name="x_bf10", align_bytes=64),
-            shared.tile([P, S], U32, name="x_bf11", align_bytes=64, offset=HALF * 4),
-        ]
-        for h, width in enumerate((HALF, WORD_SPLIT)):
-            weave(1, h, x_bf1[h][:], width)
-
-        w_bf_low = [keep.tile([P, P, PACK], BF16, name="w_bf_low%d" % z, align_bytes=64) for z in range(2)]
-        w_bf_high = keep.tile([P, 2, P, PACK], BF16, name="w_bf_high", align_bytes=64)
-        interleave(nc.scalar.copy, w_bf_low[0][:], w_raw[0, 0])
-        interleave(nc.scalar.copy, w_bf_low[1][:], w_raw[1, 0])
-        interleave(nc.scalar.copy, w_bf_high[:, 0], w_raw[0, 1])
-        nc.scalar.copy(
-            x_bf1[1][:].rearrange("p (c u) -> p c u", u=2)[:, WORD_SPLIT:, :],
-            got[1][:, 1, :, WORD_SPLIT:].rearrange("p u c -> p c u"),
-        )
-        interleave(nc.scalar.copy, w_bf_high[:, 1], w_raw[1, 1])
+        pick(scalar_gather, 1, 0, 0, S)
+        pick(scalar_gather, 1, 1, 0, S)
+        pick(nc.vector.tensor_copy, 1, 2, 0, VECTOR_PICKS)
+        pick(scalar_gather, 1, 2, VECTOR_PICKS, S)
+        pick(scalar_gather, 1, 3, 0, HALF)
+        pick(nc.vector.tensor_copy, 1, 3, HALF, S)
+        cut = HALF - SCALAR_FRAMES
+        interleave(nc.vector.tensor_copy, x_bf[1, 0][:], picked[1][:, :, halves[0]])
+        interleave(nc.scalar.copy, x_bf[1, 1][:, cut:, :], picked[1][:, :, HALF + cut : S])
+        interleave(nc.vector.tensor_copy, x_bf[1, 1][:, :cut, :], picked[1][:, :, HALF : HALF + cut])
 
         y = [keep.tile([P, S], F32, name="y%d" % m) for m in range(2)]
         acc = {(m, h): psum.tile([P, HALF], F32, name="acc%d%d" % (m, h)) for m in range(2) for h in range(2)}
 
-        def product(z, m, h):
+        def product(z, m, h, first=0):
             nc.tensor.matmul_mx(
                 out=acc[m, h][:],
                 lhsT=w_mx[z, m][0].bitcast(FP8X4),
                 lhsT_scale=w_mx[z, m][1],
                 rhs=x_mx[z, h][0].bitcast(FP8X4),
                 rhs_scale=x_mx[z, h][1],
-                start=(z == 0),
-                stop=(z == 1),
+                start=(z == first),
+                stop=(z != first),
             )
-            if z == 1:
-                nc.scalar.activation(y[m][:, halves[h]], acc[m, h][:], ACT.Gelu_apprx_tanh)
 
-        words, scales = quantize("w00", w_bf_low[0][:].rearrange("p c t -> p (c t)"), P)
-        w_mx[0, 0] = (words[:], scales[:])
+        def gelu(m, h):
+            nc.scalar.activation(y[m][:, halves[h]], acc[m, h][:], ACT.Gelu_apprx_tanh)
+
+        def round_w(copy, z, m, tag):
+            grouped = keep.tile([P, P, PACK], BF16, name="w_bf%d%d" % (z, m), tag=tag, align_bytes=64)
+            interleave(copy, grouped[:], w_raw[z][:, :, m * P : (m + 1) * P])
+            return grouped[:]
+
+        w_mx[0, 0] = quantize("w00", round_w(nc.scalar.copy, 0, 0, "w_bf00"), P)
         product(0, 0, 0)
         product(0, 0, 1)
-
-        def quantize_x1(h):
-            words = shared.tile([P, HALF], U32, name="x10_words", align_bytes=64, offset=0) if h == 0 else None
-            words, scales = quantize("x1%d" % h, x_bf1[h][:].bitcast(BF16), HALF, words)
-            x_mx[1, h] = (words[:], scales[:])
-
-        quantize_x1(0)
-        words, scales = quantize("w10", w_bf_low[1][:].rearrange("p c t -> p (c t)"), P)
-        w_mx[1, 0] = (words[:], scales[:])
-        product(1, 0, 0)
-        quantize_x1(1)
-        product(1, 0, 1)
-        rest = keep.tile([P, V], F32, name="rest", tag="w10_words", align_bytes=64)
+        for h in range(2):
+            x_mx[1, h] = quantize("x1%d" % h, x_bf[1, h][:], HALF)
+        w_mx[1, 0] = quantize("w10", round_w(nc.scalar.copy, 1, 0, "w_bf10"), P)
+        w_bf11 = round_w(nc.scalar.copy, 1, 1, "w_bf11")
+        w_bf01 = round_w(nc.vector.tensor_copy, 0, 1, "w_bf10")
+        rest = keep.tile([P, V], F32, name="rest")
         nc.scalar.activation(rest[:], frac_sb[:], ACT.Copy, bias=1.0, scale=-1.0)
-
-        words, scales = quantize("w_high", w_bf_high[:].rearrange("p z c t -> p (z c t)"), 2 * P)
-        for z in range(2):
-            w_mx[z, 1] = (words[:, z * P : (z + 1) * P], scales[:, z * P : (z + 1) * P])
-        for z in range(2):
+        for h in range(2):
+            product(1, 0, h)
+            gelu(0, h)
+        w_mx[1, 1] = quantize("w11", w_bf11, P)
+        w_mx[0, 1] = quantize("w01", w_bf01, P)
+        for z in (1, 0):
             for h in range(2):
-                product(z, 1, h)
+                product(z, 1, h, first=1)
+        for h in range(2):
+            gelu(1, h)
 
         from_right = [keep.tile([P, V], F32, name="from_right%d" % m) for m in range(2)]
         from_left = [keep.tile([P, V], F32, name="from_left%d" % m) for m in range(2)]
-        for m in range(2):
-            nc.vector.tensor_tensor(from_right[m][:], y[m][:].indirect(right_sb[:]), frac_sb[:], ALU.mult)
-            nc.vector.tensor_tensor(from_left[m][:], y[m][:].indirect(left_sb[:]), rest[:], ALU.mult)
-        for m, tag in enumerate(("frac_sb", "result1")):
+        nc.vector.tensor_tensor(from_right[0][:], y[0][:].indirect(right_sb[:]), frac_sb[:], ALU.mult)
+        nc.vector.tensor_tensor(from_left[0][:], y[0][:].indirect(left_sb[:]), rest[:], ALU.mult)
+        left_1 = [keep.tile([P, P], F32, name="left_1%d" % h) for h in range(2)]
+        for h in range(2):
+            scalar_gather(left_1[h][:], y[1][:].indirect(left_sb[:, h * (P // 16) : (h + 1) * (P // 16)]))
+        nc.vector.tensor_tensor(from_right[1][:], y[1][:].indirect(right_sb[:]), frac_sb[:], ALU.mult)
+        for h in range(2):
+            cols = slice(h * P, (h + 1) * P)
+            nc.vector.tensor_tensor(from_left[1][:, cols], left_1[h][:], rest[:, cols], ALU.mult)
+        for m, tag in enumerate(("left_10", "result1")):
             result = keep.tile([P, V], F32, name="result%d" % m, tag=tag)
             nc.vector.tensor_tensor(result[:], from_left[m][:], from_right[m][:], ALU.add)
             nc.sync.dma_start(out[m * P : (m + 1) * P, :], result[:])

@@ -19,7 +19,7 @@ PACK = 4
 K_PASS = P * PACK
 HALF = S // 2
 SCALAR_FRAMES = 96
-VECTOR_PICKS = 320
+VECTOR_PICKS = {(0, 0): 0, (0, 1): S, (0, 2): 320, (0, 3): 288, (1, 0): 0, (1, 1): 256, (1, 2): 352, (1, 3): 288}
 
 
 def interleave(copy, dst, src):
@@ -88,22 +88,22 @@ def tile_picked_lerp_gelu_e_kernel(tc, xT, w1, frac, offs, left, right, out):
         x_mx = {}
         w_mx = {}
 
-        pick(scalar_gather, 0, 0, 0, S)
-        pick(nc.vector.tensor_copy, 0, 1, 0, S)
-        pick(scalar_gather, 0, 2, 0, S)
-        pick(nc.vector.tensor_copy, 0, 3, 0, HALF)
-        pick(scalar_gather, 0, 3, HALF, S)
+        def pick_plane(z, j):
+            share = VECTOR_PICKS[z, j]
+            if share > 0:
+                pick(nc.vector.tensor_copy, z, j, 0, share)
+            if share < S:
+                pick(scalar_gather, z, j, share, S)
+
+        for j in range(PACK):
+            pick_plane(0, j)
         for h in range(2):
             interleave(nc.vector.tensor_copy, x_bf[0, h][:], picked[0][:, :, halves[h]])
         for h in range(2):
             x_mx[0, h] = quantize("x0%d" % h, x_bf[0, h][:], HALF)
 
-        pick(scalar_gather, 1, 0, 0, S)
-        pick(scalar_gather, 1, 1, 0, S)
-        pick(nc.vector.tensor_copy, 1, 2, 0, VECTOR_PICKS)
-        pick(scalar_gather, 1, 2, VECTOR_PICKS, S)
-        pick(scalar_gather, 1, 3, 0, HALF)
-        pick(nc.vector.tensor_copy, 1, 3, HALF, S)
+        for j in range(PACK):
+            pick_plane(1, j)
         cut = HALF - SCALAR_FRAMES
         interleave(nc.vector.tensor_copy, x_bf[1, 0][:], picked[1][:, :, halves[0]])
         interleave(nc.scalar.copy, x_bf[1, 1][:, cut:, :], picked[1][:, :, HALF + cut : S])

@@ -18,8 +18,9 @@ P = 128
 PACK = 4
 K_PASS = P * PACK
 HALF = S // 2
-SCALAR_FRAMES = 96
-VECTOR_PICKS = {(0, 0): 0, (0, 1): S, (0, 2): 320, (0, 3): 288, (1, 0): 0, (1, 1): 256, (1, 2): 352, (1, 3): 288}
+SCALAR_FRAMES = 144
+VECTOR_COLUMNS = (48, 64)
+VECTOR_PICKS = {(0, 0): 0, (0, 1): S, (0, 2): 256, (0, 3): 256, (1, 0): 0, (1, 1): 0, (1, 2): 320, (1, 3): 256}
 
 
 def interleave(copy, dst, src):
@@ -89,11 +90,11 @@ def tile_picked_lerp_gelu_e_kernel(tc, xT, w1, frac, offs, left, right, out):
         w_mx = {}
 
         def pick_plane(z, j):
-            share = VECTOR_PICKS[z, j]
-            if share > 0:
-                pick(nc.vector.tensor_copy, z, j, 0, share)
-            if share < S:
-                pick(scalar_gather, z, j, share, S)
+            cut = S - VECTOR_PICKS[z, j]
+            if cut > 0:
+                pick(scalar_gather, z, j, 0, cut)
+            if cut < S:
+                pick(nc.vector.tensor_copy, z, j, cut, S)
 
         for j in range(PACK):
             pick_plane(0, j)
@@ -136,8 +137,16 @@ def tile_picked_lerp_gelu_e_kernel(tc, xT, w1, frac, offs, left, right, out):
         product(0, 0, 1)
         for h in range(2):
             x_mx[1, h] = quantize("x1%d" % h, x_bf[1, h][:], HALF)
-        w_mx[1, 0] = quantize("w10", round_w(nc.scalar.copy, 1, 0, "w_bf10"), P)
-        w_bf11 = round_w(nc.scalar.copy, 1, 1, "w_bf11")
+
+        def round_shared(m):
+            grouped = keep.tile([P, P, PACK], BF16, name="w_bf1%d" % m, align_bytes=64)
+            cut = VECTOR_COLUMNS[m]
+            interleave(nc.vector.tensor_copy, grouped[:, :cut, :], w_raw[1][:, :, m * P : m * P + cut])
+            interleave(nc.scalar.copy, grouped[:, cut:, :], w_raw[1][:, :, m * P + cut : (m + 1) * P])
+            return grouped[:]
+
+        w_mx[1, 0] = quantize("w10", round_shared(0), P)
+        w_bf11 = round_shared(1)
         w_bf01 = round_w(nc.vector.tensor_copy, 0, 1, "w_bf10")
         rest = keep.tile([P, V], F32, name="rest")
         nc.scalar.activation(rest[:], frac_sb[:], ACT.Copy, bias=1.0, scale=-1.0)

@@ -20,7 +20,7 @@ K_PASS = P * PACK
 HALF = S // 2
 SCALAR_FRAMES = 144
 VECTOR_COLUMNS = (48, 64)
-VECTOR_PICKS = {(0, 0): 0, (0, 1): S, (0, 2): 256, (0, 3): 256, (1, 0): 0, (1, 1): 0, (1, 2): 320, (1, 3): 256}
+VECTOR_PICKS = {(0, 0): 0, (0, 1): S, (0, 2): 0, (0, 3): S, (1, 0): 0, (1, 1): 0, (1, 2): 288, (1, 3): 256}
 
 
 def interleave(copy, dst, src):
@@ -53,8 +53,9 @@ def tile_picked_lerp_gelu_e_kernel(tc, xT, w1, frac, offs, left, right, out):
 
         load_planes(0, 0, 2)
         nc.sync.dma_start(offs_sb[:], offs)
-        for z, j in ((0, 2), (0, 3), (1, 0), (1, 1), (1, 2), (1, 3)):
-            load_planes(z, j, 1)
+        load_planes(0, 2, 2)
+        for j in range(PACK):
+            load_planes(1, j, 1)
         w_raw = []
         for z in range(2):
             w_raw.append(keep.tile([P, PACK, N], F32, name="w_raw%d" % z, align_bytes=64))
@@ -158,21 +159,39 @@ def tile_picked_lerp_gelu_e_kernel(tc, xT, w1, frac, offs, left, right, out):
         for z in (1, 0):
             for h in range(2):
                 product(z, 1, h, first=1)
-        for h in range(2):
-            gelu(1, h)
 
         from_right = [keep.tile([P, V], F32, name="from_right%d" % m) for m in range(2)]
         from_left = [keep.tile([P, V], F32, name="from_left%d" % m) for m in range(2)]
-        nc.vector.tensor_tensor(from_right[0][:], y[0][:].indirect(right_sb[:]), frac_sb[:], ALU.mult)
-        nc.vector.tensor_tensor(from_left[0][:], y[0][:].indirect(left_sb[:]), rest[:], ALU.mult)
-        left_1 = [keep.tile([P, P], F32, name="left_1%d" % h) for h in range(2)]
+        samples = [slice(h * P, (h + 1) * P) for h in range(2)]
+        left_lists = [left_sb[:, h * (P // 16) : (h + 1) * (P // 16)] for h in range(2)]
+
+        def left_by_scalar(m, h):
+            fetched = keep.tile([P, P], F32, name="left_%d%d" % (m, h))
+            scalar_gather(fetched[:], y[m][:].indirect(left_lists[h]))
+            return fetched
+
+        def weigh_left(m, h, fetched):
+            nc.vector.tensor_tensor(from_left[m][:, samples[h]], fetched, rest[:, samples[h]], ALU.mult)
+
+        result = [keep.tile([P, V], F32, name="result%d" % m) for m in range(2)]
+
+        def add(m, h):
+            cols = samples[h]
+            nc.vector.tensor_tensor(result[m][:, cols], from_left[m][:, cols], from_right[m][:, cols], ALU.add)
+
+        left_00 = left_by_scalar(0, 0)
         for h in range(2):
-            scalar_gather(left_1[h][:], y[1][:].indirect(left_sb[:, h * (P // 16) : (h + 1) * (P // 16)]))
+            gelu(1, h)
+        nc.vector.tensor_tensor(from_right[0][:], y[0][:].indirect(right_sb[:]), frac_sb[:], ALU.mult)
+        weigh_left(0, 1, y[0][:].indirect(left_lists[1]))
+        weigh_left(0, 0, left_00[:])
+        add(0, 1)
+        add(0, 0)
+        nc.sync.dma_start(out[0:P, :], result[0][:])
+        left_1 = [left_by_scalar(1, h) for h in range(2)]
         nc.vector.tensor_tensor(from_right[1][:], y[1][:].indirect(right_sb[:]), frac_sb[:], ALU.mult)
         for h in range(2):
-            cols = slice(h * P, (h + 1) * P)
-            nc.vector.tensor_tensor(from_left[1][:, cols], left_1[h][:], rest[:, cols], ALU.mult)
-        for m, tag in enumerate(("left_10", "result1")):
-            result = keep.tile([P, V], F32, name="result%d" % m, tag=tag)
-            nc.vector.tensor_tensor(result[:], from_left[m][:], from_right[m][:], ALU.add)
-            nc.sync.dma_start(out[m * P : (m + 1) * P, :], result[:])
+            weigh_left(1, h, left_1[h][:])
+        for h in range(2):
+            add(1, h)
+            nc.sync.dma_start(out[P:N, samples[h]], result[1][:, samples[h]])

@@ -112,21 +112,29 @@ def tile_picked_lerp_gelu_e_kernel(tc, xT, w1, frac, offs, left, right, out):
         interleave(nc.vector.tensor_copy, x_bf[1, 1][:, :cut, :], picked[1][:, :, HALF : HALF + cut])
 
         y = [keep.tile([P, S], F32, name="y%d" % m) for m in range(2)]
-        acc = {(m, h): psum.tile([P, HALF], F32, name="acc%d%d" % (m, h)) for m in range(2) for h in range(2)}
+        widths = (S // 4, HALF)
+        acc = {
+            (m, first): psum.tile([P, widths[m]], F32, name="acc%d_%d" % (m, first))
+            for m in range(2)
+            for first in range(0, S, widths[m])
+        }
 
-        def product(z, m, h, first=0):
-            nc.tensor.matmul_mx(
-                out=acc[m, h][:],
-                lhsT=w_mx[z, m][0].bitcast(FP8X4),
-                lhsT_scale=w_mx[z, m][1],
-                rhs=x_mx[z, h][0].bitcast(FP8X4),
-                rhs_scale=x_mx[z, h][1],
-                start=(z == first),
-                stop=(z != first),
-            )
+        def product(z, m, h, first_pass=0):
+            for first in range(h * HALF, (h + 1) * HALF, widths[m]):
+                cols = slice(first - h * HALF, first - h * HALF + widths[m])
+                nc.tensor.matmul_mx(
+                    out=acc[m, first][:],
+                    lhsT=w_mx[z, m][0].bitcast(FP8X4),
+                    lhsT_scale=w_mx[z, m][1],
+                    rhs=x_mx[z, h][0][:, cols].bitcast(FP8X4),
+                    rhs_scale=x_mx[z, h][1][:, cols],
+                    start=(z == first_pass),
+                    stop=(z != first_pass),
+                )
 
         def gelu(m, h):
-            nc.scalar.activation(y[m][:, halves[h]], acc[m, h][:], ACT.Gelu_apprx_tanh)
+            for first in range(h * HALF, (h + 1) * HALF, widths[m]):
+                nc.scalar.activation(y[m][:, first : first + widths[m]], acc[m, first][:], ACT.Gelu_apprx_tanh)
 
         def round_w(copy, z, m, tag):
             grouped = keep.tile([P, P, PACK], BF16, name="w_bf%d%d" % (z, m), tag=tag, align_bytes=64)
@@ -158,7 +166,7 @@ def tile_picked_lerp_gelu_e_kernel(tc, xT, w1, frac, offs, left, right, out):
         w_mx[0, 1] = quantize("w01", w_bf01, P)
         for z in (1, 0):
             for h in range(2):
-                product(z, 1, h, first=1)
+                product(z, 1, h, first_pass=1)
 
         from_right = [keep.tile([P, V], F32, name="from_right%d" % m) for m in range(2)]
         from_left = [keep.tile([P, V], F32, name="from_left%d" % m) for m in range(2)]

@@ -18,8 +18,7 @@ P = 128
 PACK = 4
 K_PASS = P * PACK
 HALF = S // 2
-SCALAR_FRAMES = 144
-VECTOR_COLUMNS = (48, 64)
+VECTOR_COLUMNS = {(1, 0): 40, (0, 1): 64, (1, 1): 64}
 VECTOR_PICKS = {(0, 0): 0, (0, 1): S, (0, 2): 0, (0, 3): S, (1, 0): 0, (1, 1): 0, (1, 2): 288, (1, 3): 256}
 
 
@@ -56,14 +55,18 @@ def tile_picked_lerp_gelu_e_kernel(tc, xT, w1, frac, offs, left, right, out):
         load_planes(0, 2, 2)
         for j in range(PACK):
             load_planes(1, j, 1)
-        w_raw = []
-        for z in range(2):
-            w_raw.append(keep.tile([P, PACK, N], F32, name="w_raw%d" % z, align_bytes=64))
-            nc.sync.dma_start(w_raw[z][:], w1[z * K_PASS : (z + 1) * K_PASS, :].rearrange("(p j) m -> p j m", j=PACK))
+        w_rows = w1.rearrange("(z p j) m -> z p j m", p=P, j=PACK)
+        w_first = keep.tile([P, PACK, N], F32, name="w_first", align_bytes=64)
+        nc.sync.dma_start(w_first[:], w_rows[0])
+        w_raw = {(0, m): w_first[:, :, m * P : (m + 1) * P] for m in range(2)}
+        for m in range(2):
+            raw = keep.tile([P, PACK, P], F32, name="w_raw1%d" % m, align_bytes=64)
+            nc.sync.dma_start(raw[:], w_rows[1, :, :, m * P : (m + 1) * P])
+            w_raw[1, m] = raw[:]
         frac_sb = keep.tile([P, V], F32, name="frac_sb")
         nc.sync.dma_start(frac_sb[:], frac)
-        nc.sync.dma_start(right_sb[:], right)
         nc.sync.dma_start(left_sb[:], left)
+        nc.sync.dma_start(right_sb[:], right)
 
         halves = [slice(h * HALF, (h + 1) * HALF) for h in range(2)]
         picked = [keep.tile([P, PACK, S], F32, name="picked%d" % z, align_bytes=64) for z in range(2)]
@@ -106,10 +109,8 @@ def tile_picked_lerp_gelu_e_kernel(tc, xT, w1, frac, offs, left, right, out):
 
         for j in range(PACK):
             pick_plane(1, j)
-        cut = HALF - SCALAR_FRAMES
         interleave(nc.vector.tensor_copy, x_bf[1, 0][:], picked[1][:, :, halves[0]])
-        interleave(nc.scalar.copy, x_bf[1, 1][:, cut:, :], picked[1][:, :, HALF + cut : S])
-        interleave(nc.vector.tensor_copy, x_bf[1, 1][:, :cut, :], picked[1][:, :, HALF : HALF + cut])
+        interleave(nc.scalar.copy, x_bf[1, 1][:], picked[1][:, :, halves[1]])
 
         y = [keep.tile([P, S], F32, name="y%d" % m) for m in range(2)]
         widths = (S // 4, HALF)
@@ -119,7 +120,7 @@ def tile_picked_lerp_gelu_e_kernel(tc, xT, w1, frac, offs, left, right, out):
             for first in range(0, S, widths[m])
         }
 
-        def product(z, m, h, first_pass=0):
+        def product(z, m, h):
             for first in range(h * HALF, (h + 1) * HALF, widths[m]):
                 cols = slice(first - h * HALF, first - h * HALF + widths[m])
                 nc.tensor.matmul_mx(
@@ -128,8 +129,8 @@ def tile_picked_lerp_gelu_e_kernel(tc, xT, w1, frac, offs, left, right, out):
                     lhsT_scale=w_mx[z, m][1],
                     rhs=x_mx[z, h][0][:, cols].bitcast(FP8X4),
                     rhs_scale=x_mx[z, h][1][:, cols],
-                    start=(z == first_pass),
-                    stop=(z != first_pass),
+                    start=(z == 0),
+                    stop=(z == 1),
                 )
 
         def gelu(m, h):
@@ -138,35 +139,37 @@ def tile_picked_lerp_gelu_e_kernel(tc, xT, w1, frac, offs, left, right, out):
 
         def round_w(copy, z, m, tag):
             grouped = keep.tile([P, P, PACK], BF16, name="w_bf%d%d" % (z, m), tag=tag, align_bytes=64)
-            interleave(copy, grouped[:], w_raw[z][:, :, m * P : (m + 1) * P])
+            interleave(copy, grouped[:], w_raw[z, m])
             return grouped[:]
 
-        w_mx[0, 0] = quantize("w00", round_w(nc.scalar.copy, 0, 0, "w_bf00"), P)
+        w_bf00 = round_w(nc.vector.tensor_copy, 0, 0, "w_bf00")
+        x_mx[1, 0] = quantize("x10", x_bf[1, 0][:], HALF)
+        w_mx[0, 0] = quantize("w00", w_bf00, P)
         product(0, 0, 0)
         product(0, 0, 1)
-        for h in range(2):
-            x_mx[1, h] = quantize("x1%d" % h, x_bf[1, h][:], HALF)
 
-        def round_shared(m):
-            grouped = keep.tile([P, P, PACK], BF16, name="w_bf1%d" % m, align_bytes=64)
-            cut = VECTOR_COLUMNS[m]
-            interleave(nc.vector.tensor_copy, grouped[:, :cut, :], w_raw[1][:, :, m * P : m * P + cut])
-            interleave(nc.scalar.copy, grouped[:, cut:, :], w_raw[1][:, :, m * P + cut : (m + 1) * P])
+        def round_shared(z, m, tag):
+            grouped = keep.tile([P, P, PACK], BF16, name="w_bf%d%d" % (z, m), tag=tag, align_bytes=64)
+            cut = VECTOR_COLUMNS[z, m]
+            interleave(nc.vector.tensor_copy, grouped[:, :cut, :], w_raw[z, m][:, :, :cut])
+            interleave(nc.scalar.copy, grouped[:, cut:, :], w_raw[z, m][:, :, cut:])
             return grouped[:]
 
-        w_mx[1, 0] = quantize("w10", round_shared(0), P)
-        w_bf11 = round_shared(1)
-        w_bf01 = round_w(nc.vector.tensor_copy, 0, 1, "w_bf10")
-        rest = keep.tile([P, V], F32, name="rest")
-        nc.scalar.activation(rest[:], frac_sb[:], ACT.Copy, bias=1.0, scale=-1.0)
+        w_bf10 = round_shared(1, 0, "w_bf10")
+        x_mx[1, 1] = quantize("x11", x_bf[1, 1][:], HALF)
+        w_mx[1, 0] = quantize("w10", w_bf10, P)
+        w_bf01 = round_shared(0, 1, "w_raw10")
+        w_bf11 = round_shared(1, 1, "w_bf11")
         for h in range(2):
             product(1, 0, h)
             gelu(0, h)
-        w_mx[1, 1] = quantize("w11", w_bf11, P)
         w_mx[0, 1] = quantize("w01", w_bf01, P)
-        for z in (1, 0):
+        w_mx[1, 1] = quantize("w11", w_bf11, P)
+        rest = keep.tile([P, V], F32, name="rest")
+        nc.vector.tensor_scalar(rest[:], frac_sb[:], -1.0, 1.0, ALU.mult, ALU.add)
+        for z in range(2):
             for h in range(2):
-                product(z, 1, h, first_pass=1)
+                product(z, 1, h)
 
         from_right = [keep.tile([P, V], F32, name="from_right%d" % m) for m in range(2)]
         from_left = [keep.tile([P, V], F32, name="from_left%d" % m) for m in range(2)]
@@ -183,23 +186,19 @@ def tile_picked_lerp_gelu_e_kernel(tc, xT, w1, frac, offs, left, right, out):
 
         result = [keep.tile([P, V], F32, name="result%d" % m) for m in range(2)]
 
-        def add(m, h):
-            cols = samples[h]
-            nc.vector.tensor_tensor(result[m][:, cols], from_left[m][:, cols], from_right[m][:, cols], ALU.add)
-
         left_00 = left_by_scalar(0, 0)
         for h in range(2):
             gelu(1, h)
-        nc.vector.tensor_tensor(from_right[0][:], y[0][:].indirect(right_sb[:]), frac_sb[:], ALU.mult)
         weigh_left(0, 1, y[0][:].indirect(left_lists[1]))
         weigh_left(0, 0, left_00[:])
-        add(0, 1)
-        add(0, 0)
+        nc.vector.tensor_tensor(from_right[0][:], y[0][:].indirect(right_sb[:]), frac_sb[:], ALU.mult)
+        nc.vector.tensor_tensor(result[0][:], from_left[0][:], from_right[0][:], ALU.add)
         nc.sync.dma_start(out[0:P, :], result[0][:])
         left_1 = [left_by_scalar(1, h) for h in range(2)]
         nc.vector.tensor_tensor(from_right[1][:], y[1][:].indirect(right_sb[:]), frac_sb[:], ALU.mult)
         for h in range(2):
             weigh_left(1, h, left_1[h][:])
         for h in range(2):
-            add(1, h)
+            cols = samples[h]
+            nc.vector.tensor_tensor(result[1][:, cols], from_left[1][:, cols], from_right[1][:, cols], ALU.add)
             nc.sync.dma_start(out[P:N, samples[h]], result[1][:, samples[h]])

@@ -18,7 +18,7 @@ P = 128
 PACK = 4
 K_PASS = P * PACK
 HALF = S // 2
-VECTOR_COLUMNS = {(1, 0): 40, (0, 1): 64, (1, 1): 64}
+VECTOR_COLUMNS = {(0, 1): 32, (1, 1): 64}
 VECTOR_PICKS = {(0, 0): 0, (0, 1): S, (0, 2): 0, (0, 3): S, (1, 0): 0, (1, 1): 0, (1, 2): 288, (1, 3): 256}
 
 
@@ -56,13 +56,12 @@ def tile_picked_lerp_gelu_e_kernel(tc, xT, w1, frac, offs, left, right, out):
         for j in range(PACK):
             load_planes(1, j, 1)
         w_rows = w1.rearrange("(z p j) m -> z p j m", p=P, j=PACK)
-        w_first = keep.tile([P, PACK, N], F32, name="w_first", align_bytes=64)
-        nc.sync.dma_start(w_first[:], w_rows[0])
-        w_raw = {(0, m): w_first[:, :, m * P : (m + 1) * P] for m in range(2)}
+        w_raw = {}
         for m in range(2):
-            raw = keep.tile([P, PACK, P], F32, name="w_raw1%d" % m, align_bytes=64)
-            nc.sync.dma_start(raw[:], w_rows[1, :, :, m * P : (m + 1) * P])
-            w_raw[1, m] = raw[:]
+            for z in range(2):
+                raw = keep.tile([P, PACK, P], F32, name="w_raw%d%d" % (z, m), align_bytes=64)
+                nc.sync.dma_start(raw[:], w_rows[z, :, :, m * P : (m + 1) * P])
+                w_raw[z, m] = raw[:]
         frac_sb = keep.tile([P, V], F32, name="frac_sb")
         nc.sync.dma_start(frac_sb[:], frac)
         nc.sync.dma_start(left_sb[:], left)
@@ -87,8 +86,7 @@ def tile_picked_lerp_gelu_e_kernel(tc, xT, w1, frac, offs, left, right, out):
 
         x_bf = {
             (z, h): keep.tile([P, HALF, PACK], BF16, name="x_bf%d%d" % (z, h), align_bytes=64)
-            for z in range(2)
-            for h in range(2)
+            for z, h in ((0, 0), (0, 1), (1, 0))
         }
         x_mx = {}
         w_mx = {}
@@ -109,11 +107,9 @@ def tile_picked_lerp_gelu_e_kernel(tc, xT, w1, frac, offs, left, right, out):
 
         for j in range(PACK):
             pick_plane(1, j)
-        interleave(nc.vector.tensor_copy, x_bf[1, 0][:], picked[1][:, :, halves[0]])
-        interleave(nc.scalar.copy, x_bf[1, 1][:], picked[1][:, :, halves[1]])
 
         y = [keep.tile([P, S], F32, name="y%d" % m) for m in range(2)]
-        widths = (S // 4, HALF)
+        widths = (S // 4, S // 4)
         acc = {
             (m, first): psum.tile([P, widths[m]], F32, name="acc%d_%d" % (m, first))
             for m in range(2)
@@ -142,12 +138,6 @@ def tile_picked_lerp_gelu_e_kernel(tc, xT, w1, frac, offs, left, right, out):
             interleave(copy, grouped[:], w_raw[z, m])
             return grouped[:]
 
-        w_bf00 = round_w(nc.vector.tensor_copy, 0, 0, "w_bf00")
-        x_mx[1, 0] = quantize("x10", x_bf[1, 0][:], HALF)
-        w_mx[0, 0] = quantize("w00", w_bf00, P)
-        product(0, 0, 0)
-        product(0, 0, 1)
-
         def round_shared(z, m, tag):
             grouped = keep.tile([P, P, PACK], BF16, name="w_bf%d%d" % (z, m), tag=tag, align_bytes=64)
             cut = VECTOR_COLUMNS[z, m]
@@ -155,18 +145,49 @@ def tile_picked_lerp_gelu_e_kernel(tc, xT, w1, frac, offs, left, right, out):
             interleave(nc.scalar.copy, grouped[:, cut:, :], w_raw[z, m][:, :, cut:])
             return grouped[:]
 
-        w_bf10 = round_shared(1, 0, "w_bf10")
-        x_mx[1, 1] = quantize("x11", x_bf[1, 1][:], HALF)
+        def lay_piece(copy, first, last, tag):
+            grouped = keep.tile([P, last - first, PACK], BF16, name="x_bf_%d" % first, tag=tag, align_bytes=64)
+            interleave(copy, grouped[:], picked[1][:, :, first:last])
+            return grouped[:]
+
+        last_words = keep.tile([P, HALF], U32, name="x11_words", align_bytes=64)
+        last_scales = keep.tile([P, HALF], U8, name="x11_scales", align_bytes=64)
+        x_mx[1, 1] = (last_words[:], last_scales[:])
+
+        def quantize_piece(grouped, first, last):
+            cols = slice(first - HALF, last - HALF)
+            nc.vector.quantize_mx(
+                out=last_words[:, cols].bitcast(FP8X4),
+                scales=last_scales[:, cols],
+                in_=grouped.rearrange("p c t -> p (c t)"),
+            )
+
+        quarter = S // 4
+        interleave(nc.vector.tensor_copy, x_bf[1, 0][:, :quarter, :], picked[1][:, :, :quarter])
+        piece_c = lay_piece(nc.scalar.copy, 256, 384, "x_bf_c")
+        w_bf00 = round_w(nc.vector.tensor_copy, 0, 0, "w_bf00")
+        interleave(nc.vector.tensor_copy, x_bf[1, 0][:, quarter:, :], picked[1][:, :, quarter:HALF])
+        w_mx[0, 0] = quantize("w00", w_bf00, P)
+        product(0, 0, 0)
+        product(0, 0, 1)
+        piece_d = lay_piece(nc.vector.tensor_copy, 384, 448, "x_bf_d")
+        w_bf10 = round_w(nc.scalar.copy, 1, 0, "w_bf10")
+        piece_e = lay_piece(nc.scalar.copy, 448, 512, "w_raw10")
+        x_mx[1, 0] = quantize("x10", x_bf[1, 0][:], HALF)
         w_mx[1, 0] = quantize("w10", w_bf10, P)
-        w_bf01 = round_shared(0, 1, "w_raw10")
+        w_bf01 = round_shared(0, 1, "w_bf01")
+        quantize_piece(piece_c, 256, 384)
+        quantize_piece(piece_d, 384, 448)
+        quantize_piece(piece_e, 448, 512)
+        w_mx[0, 1] = quantize("w01", w_bf01, P)
+
         w_bf11 = round_shared(1, 1, "w_bf11")
         for h in range(2):
             product(1, 0, h)
             gelu(0, h)
-        w_mx[0, 1] = quantize("w01", w_bf01, P)
-        w_mx[1, 1] = quantize("w11", w_bf11, P)
         rest = keep.tile([P, V], F32, name="rest")
         nc.vector.tensor_scalar(rest[:], frac_sb[:], -1.0, 1.0, ALU.mult, ALU.add)
+        w_mx[1, 1] = quantize("w11", w_bf11, P)
         for z in range(2):
             for h in range(2):
                 product(z, 1, h)
@@ -186,11 +207,9 @@ def tile_picked_lerp_gelu_e_kernel(tc, xT, w1, frac, offs, left, right, out):
 
         result = [keep.tile([P, V], F32, name="result%d" % m) for m in range(2)]
 
-        left_00 = left_by_scalar(0, 0)
         for h in range(2):
             gelu(1, h)
-        weigh_left(0, 1, y[0][:].indirect(left_lists[1]))
-        weigh_left(0, 0, left_00[:])
+        nc.vector.tensor_tensor(from_left[0][:], y[0][:].indirect(left_sb[:]), rest[:], ALU.mult)
         nc.vector.tensor_tensor(from_right[0][:], y[0][:].indirect(right_sb[:]), frac_sb[:], ALU.mult)
         nc.vector.tensor_tensor(result[0][:], from_left[0][:], from_right[0][:], ALU.add)
         nc.sync.dma_start(out[0:P, :], result[0][:])
@@ -201,4 +220,4 @@ def tile_picked_lerp_gelu_e_kernel(tc, xT, w1, frac, offs, left, right, out):
         for h in range(2):
             cols = samples[h]
             nc.vector.tensor_tensor(result[1][:, cols], from_left[1][:, cols], from_right[1][:, cols], ALU.add)
-            nc.sync.dma_start(out[P:N, samples[h]], result[1][:, samples[h]])
+        nc.sync.dma_start(out[P:N, :], result[1][:])

@@ -16,10 +16,12 @@ ALU = mybir.AluOpType
 
 P = 128
 PACK = 4
-K_PASS = P * PACK
 HALF = S // 2
-VECTOR_COLUMNS = {(0, 1): 32, (1, 1): 64}
-VECTOR_PICKS = {(0, 0): 0, (0, 1): S, (0, 2): 0, (0, 3): S, (1, 0): 0, (1, 1): 0, (1, 2): 288, (1, 3): 256}
+QUARTER = S // 4
+THIRD_PLANE_CUT = 224
+LAST_PLANE_CUT = 320
+VECTOR_COLUMNS = 80
+QUARTER_ORDER = (0, 1, 3, 2)
 
 
 def interleave(copy, dst, src):
@@ -67,7 +69,6 @@ def tile_picked_lerp_gelu_e_kernel(tc, xT, w1, frac, offs, left, right, out):
         nc.sync.dma_start(left_sb[:], left)
         nc.sync.dma_start(right_sb[:], right)
 
-        halves = [slice(h * HALF, (h + 1) * HALF) for h in range(2)]
         picked = [keep.tile([P, PACK, S], F32, name="picked%d" % z, align_bytes=64) for z in range(2)]
 
         def scalar_gather(dst, src):
@@ -76,7 +77,13 @@ def tile_picked_lerp_gelu_e_kernel(tc, xT, w1, frac, offs, left, right, out):
         def pick(copy, z, j, first, last):
             copy(picked[z][:, j, first:last], plane[z, j].indirect(offs_sb[:, first // 16 : last // 16]))
 
-        def quantize(name, grouped, n):
+        def lay(copy, name, src):
+            grouped = keep.tile([P, src.shape[2], PACK], BF16, name=name, align_bytes=64)
+            interleave(copy, grouped[:], src)
+            return grouped[:]
+
+        def quantize(name, grouped):
+            n = grouped.shape[1]
             words = keep.tile([P, n], U32, name=name + "_words", align_bytes=64)
             scales = keep.tile([P, n], U8, name=name + "_scales", align_bytes=64)
             nc.vector.quantize_mx(
@@ -84,140 +91,90 @@ def tile_picked_lerp_gelu_e_kernel(tc, xT, w1, frac, offs, left, right, out):
             )
             return words[:], scales[:]
 
-        x_bf = {
-            (z, h): keep.tile([P, HALF, PACK], BF16, name="x_bf%d%d" % (z, h), align_bytes=64)
-            for z, h in ((0, 0), (0, 1), (1, 0))
-        }
         x_mx = {}
         w_mx = {}
 
-        def pick_plane(z, j):
-            cut = S - VECTOR_PICKS[z, j]
-            if cut > 0:
-                pick(scalar_gather, z, j, 0, cut)
-            if cut < S:
-                pick(nc.vector.tensor_copy, z, j, cut, S)
-
         for j in range(PACK):
-            pick_plane(0, j)
+            pick(nc.vector.tensor_copy if j % 2 else scalar_gather, 0, j, 0, S)
+        laid = [lay(nc.vector.tensor_copy, "x_bf0%d" % h, picked[0][:, :, h * HALF : (h + 1) * HALF]) for h in range(2)]
         for h in range(2):
-            interleave(nc.vector.tensor_copy, x_bf[0, h][:], picked[0][:, :, halves[h]])
-        for h in range(2):
-            x_mx[0, h] = quantize("x0%d" % h, x_bf[0, h][:], HALF)
+            words, scales = quantize("x0%d" % h, laid[h])
+            for q in range(2):
+                cols = slice(q * QUARTER, (q + 1) * QUARTER)
+                x_mx[0, 2 * h + q] = (words[:, cols], scales[:, cols])
 
-        for j in range(PACK):
-            pick_plane(1, j)
+        pick(scalar_gather, 1, 0, 0, S)
+        pick(scalar_gather, 1, 1, 0, S)
+        pick(scalar_gather, 1, 2, 0, THIRD_PLANE_CUT)
+        pick(nc.vector.tensor_copy, 1, 2, THIRD_PLANE_CUT, S)
+        pick(scalar_gather, 1, 3, 0, QUARTER)
+        pick(nc.vector.tensor_copy, 1, 3, LAST_PLANE_CUT, S)
+        pick(scalar_gather, 1, 3, QUARTER, LAST_PLANE_CUT)
 
         y = [keep.tile([P, S], F32, name="y%d" % m) for m in range(2)]
-        widths = (S // 4, S // 4)
-        acc = {
-            (m, first): psum.tile([P, widths[m]], F32, name="acc%d_%d" % (m, first))
-            for m in range(2)
-            for first in range(0, S, widths[m])
-        }
+        acc = {(m, q): psum.tile([P, QUARTER], F32, name="acc%d%d" % (m, q)) for m in range(2) for q in range(4)}
 
-        def product(z, m, h):
-            for first in range(h * HALF, (h + 1) * HALF, widths[m]):
-                cols = slice(first - h * HALF, first - h * HALF + widths[m])
+        def products(z, m, quarters):
+            for q in quarters:
                 nc.tensor.matmul_mx(
-                    out=acc[m, first][:],
+                    out=acc[m, q][:],
                     lhsT=w_mx[z, m][0].bitcast(FP8X4),
                     lhsT_scale=w_mx[z, m][1],
-                    rhs=x_mx[z, h][0][:, cols].bitcast(FP8X4),
-                    rhs_scale=x_mx[z, h][1][:, cols],
+                    rhs=x_mx[z, q][0].bitcast(FP8X4),
+                    rhs_scale=x_mx[z, q][1],
                     start=(z == 0),
                     stop=(z == 1),
                 )
 
-        def gelu(m, h):
-            for first in range(h * HALF, (h + 1) * HALF, widths[m]):
-                nc.scalar.activation(y[m][:, first : first + widths[m]], acc[m, first][:], ACT.Gelu_apprx_tanh)
+        def gelus(m, quarters):
+            for q in quarters:
+                nc.scalar.activation(y[m][:, q * QUARTER : (q + 1) * QUARTER], acc[m, q][:], ACT.Gelu_apprx_tanh)
 
-        def round_w(copy, z, m, tag):
-            grouped = keep.tile([P, P, PACK], BF16, name="w_bf%d%d" % (z, m), tag=tag, align_bytes=64)
-            interleave(copy, grouped[:], w_raw[z, m])
-            return grouped[:]
+        def lay_quarter(copy, q):
+            return lay(copy, "x_bf1%d" % q, picked[1][:, :, q * QUARTER : (q + 1) * QUARTER])
 
-        def round_shared(z, m, tag):
-            grouped = keep.tile([P, P, PACK], BF16, name="w_bf%d%d" % (z, m), tag=tag, align_bytes=64)
-            cut = VECTOR_COLUMNS[z, m]
-            interleave(nc.vector.tensor_copy, grouped[:, :cut, :], w_raw[z, m][:, :, :cut])
-            interleave(nc.scalar.copy, grouped[:, cut:, :], w_raw[z, m][:, :, cut:])
-            return grouped[:]
+        x_bf = {0: lay_quarter(nc.vector.tensor_copy, 0), 3: lay_quarter(nc.scalar.copy, 3)}
+        w_bf00 = lay(nc.vector.tensor_copy, "w_bf00", w_raw[0, 0])
+        x_bf[1] = lay_quarter(nc.vector.tensor_copy, 1)
+        w_mx[0, 0] = quantize("w00", w_bf00)
+        products(0, 0, QUARTER_ORDER)
+        x_bf[2] = lay_quarter(nc.vector.tensor_copy, 2)
+        w_bf10 = lay(nc.scalar.copy, "w_bf10", w_raw[1, 0])
+        x_mx[1, 0] = quantize("x10", x_bf[0])
+        w_mx[1, 0] = quantize("w10", w_bf10)
+        w_bf01 = lay(nc.scalar.copy, "w_bf01", w_raw[0, 1])
+        for q in QUARTER_ORDER[1:]:
+            x_mx[1, q] = quantize("x1%d" % q, x_bf[q])
+        w_mx[0, 1] = quantize("w01", w_bf01)
 
-        def lay_piece(copy, first, last, tag):
-            grouped = keep.tile([P, last - first, PACK], BF16, name="x_bf_%d" % first, tag=tag, align_bytes=64)
-            interleave(copy, grouped[:], picked[1][:, :, first:last])
-            return grouped[:]
-
-        last_words = keep.tile([P, HALF], U32, name="x11_words", align_bytes=64)
-        last_scales = keep.tile([P, HALF], U8, name="x11_scales", align_bytes=64)
-        x_mx[1, 1] = (last_words[:], last_scales[:])
-
-        def quantize_piece(grouped, first, last):
-            cols = slice(first - HALF, last - HALF)
-            nc.vector.quantize_mx(
-                out=last_words[:, cols].bitcast(FP8X4),
-                scales=last_scales[:, cols],
-                in_=grouped.rearrange("p c t -> p (c t)"),
-            )
-
-        quarter = S // 4
-        interleave(nc.vector.tensor_copy, x_bf[1, 0][:, :quarter, :], picked[1][:, :, :quarter])
-        piece_c = lay_piece(nc.scalar.copy, 256, 384, "x_bf_c")
-        w_bf00 = round_w(nc.vector.tensor_copy, 0, 0, "w_bf00")
-        interleave(nc.vector.tensor_copy, x_bf[1, 0][:, quarter:, :], picked[1][:, :, quarter:HALF])
-        w_mx[0, 0] = quantize("w00", w_bf00, P)
-        product(0, 0, 0)
-        product(0, 0, 1)
-        piece_d = lay_piece(nc.vector.tensor_copy, 384, 448, "x_bf_d")
-        w_bf10 = round_w(nc.scalar.copy, 1, 0, "w_bf10")
-        piece_e = lay_piece(nc.scalar.copy, 448, 512, "w_raw10")
-        x_mx[1, 0] = quantize("x10", x_bf[1, 0][:], HALF)
-        w_mx[1, 0] = quantize("w10", w_bf10, P)
-        w_bf01 = round_shared(0, 1, "w_bf01")
-        quantize_piece(piece_c, 256, 384)
-        quantize_piece(piece_d, 384, 448)
-        quantize_piece(piece_e, 448, 512)
-        w_mx[0, 1] = quantize("w01", w_bf01, P)
-
-        w_bf11 = round_shared(1, 1, "w_bf11")
-        for h in range(2):
-            product(1, 0, h)
-            gelu(0, h)
+        w_bf11 = keep.tile([P, P, PACK], BF16, name="w_bf11", align_bytes=64)
+        interleave(nc.vector.tensor_copy, w_bf11[:, :VECTOR_COLUMNS, :], w_raw[1, 1][:, :, :VECTOR_COLUMNS])
+        interleave(nc.scalar.copy, w_bf11[:, VECTOR_COLUMNS:, :], w_raw[1, 1][:, :, VECTOR_COLUMNS:])
+        for pair in (QUARTER_ORDER[:2], QUARTER_ORDER[2:]):
+            products(1, 0, pair)
+            gelus(0, pair)
         rest = keep.tile([P, V], F32, name="rest")
         nc.vector.tensor_scalar(rest[:], frac_sb[:], -1.0, 1.0, ALU.mult, ALU.add)
-        w_mx[1, 1] = quantize("w11", w_bf11, P)
+        w_mx[1, 1] = quantize("w11", w_bf11[:])
         for z in range(2):
-            for h in range(2):
-                product(z, 1, h)
+            products(z, 1, QUARTER_ORDER)
 
         from_right = [keep.tile([P, V], F32, name="from_right%d" % m) for m in range(2)]
         from_left = [keep.tile([P, V], F32, name="from_left%d" % m) for m in range(2)]
-        samples = [slice(h * P, (h + 1) * P) for h in range(2)]
-        left_lists = [left_sb[:, h * (P // 16) : (h + 1) * (P // 16)] for h in range(2)]
-
-        def left_by_scalar(m, h):
-            fetched = keep.tile([P, P], F32, name="left_%d%d" % (m, h))
-            scalar_gather(fetched[:], y[m][:].indirect(left_lists[h]))
-            return fetched
-
-        def weigh_left(m, h, fetched):
-            nc.vector.tensor_tensor(from_left[m][:, samples[h]], fetched, rest[:, samples[h]], ALU.mult)
-
         result = [keep.tile([P, V], F32, name="result%d" % m) for m in range(2)]
+        samples = [slice(h * P, (h + 1) * P) for h in range(2)]
 
-        for h in range(2):
-            gelu(1, h)
+        gelus(1, QUARTER_ORDER)
         nc.vector.tensor_tensor(from_left[0][:], y[0][:].indirect(left_sb[:]), rest[:], ALU.mult)
         nc.vector.tensor_tensor(from_right[0][:], y[0][:].indirect(right_sb[:]), frac_sb[:], ALU.mult)
         nc.vector.tensor_tensor(result[0][:], from_left[0][:], from_right[0][:], ALU.add)
         nc.sync.dma_start(out[0:P, :], result[0][:])
-        left_1 = [left_by_scalar(1, h) for h in range(2)]
+        fetched = [keep.tile([P, P], F32, name="left_1%d" % h) for h in range(2)]
+        for h in range(2):
+            scalar_gather(fetched[h][:], y[1][:].indirect(left_sb[:, h * (P // 16) : (h + 1) * (P // 16)]))
         nc.vector.tensor_tensor(from_right[1][:], y[1][:].indirect(right_sb[:]), frac_sb[:], ALU.mult)
         for h in range(2):
-            weigh_left(1, h, left_1[h][:])
-        for h in range(2):
-            cols = samples[h]
+            nc.vector.tensor_tensor(from_left[1][:, samples[h]], fetched[h][:], rest[:, samples[h]], ALU.mult)
+        for cols in samples:
             nc.vector.tensor_tensor(result[1][:, cols], from_left[1][:, cols], from_right[1][:, cols], ALU.add)
         nc.sync.dma_start(out[P:N, :], result[1][:])

@@ -18,10 +18,9 @@ P = 128
 PACK = 4
 HALF = S // 2
 QUARTER = S // 4
-THIRD_PLANE_CUT = 224
-LAST_PLANE_CUT = 320
-VECTOR_COLUMNS = 80
-QUARTER_ORDER = (0, 1, 3, 2)
+EARLY_CUT = 192
+LATE_CUT = 320
+QUARTER_ORDER = (3, 0, 1, 2)
 
 
 def interleave(copy, dst, src):
@@ -44,78 +43,71 @@ def tile_picked_lerp_gelu_e_kernel(tc, xT, w1, frac, offs, left, right, out):
         nc.scalar.activation(warm_out[:], warm[:], ACT.Gelu_apprx_tanh)
 
         x_rows = xT.rearrange("(z p j) t -> z p j t", p=P, j=PACK)
-        plane = {}
-
-        def load_planes(z, first, count):
-            raw = keep.tile([P, count, T], F32, name="raw%d%d" % (z, first), align_bytes=64)
-            nc.sync.dma_start(raw[:], x_rows[z, :, first : first + count, :])
-            for j in range(count):
-                plane[z, first + j] = raw[:, j, :]
-
-        load_planes(0, 0, 2)
-        nc.sync.dma_start(offs_sb[:], offs)
-        load_planes(0, 2, 2)
+        pair = []
+        for j in range(2):
+            raw = keep.tile([P, 2 * T], F32, name="pair%d" % j, align_bytes=256)
+            nc.sync.dma_start(raw[:].rearrange("p (u t) -> p u t", u=2), x_rows[0, :, j:PACK:2, :])
+            pair.append(raw)
+            if j == 0:
+                nc.sync.dma_start(offs_sb[:], offs)
+        plane = []
         for j in range(PACK):
-            load_planes(1, j, 1)
+            raw = keep.tile([P, T], F32, name="plane%d" % j, align_bytes=256)
+            nc.sync.dma_start(raw[:], x_rows[1, :, j, :])
+            plane.append(raw)
         w_rows = w1.rearrange("(z p j) m -> z p j m", p=P, j=PACK)
         w_raw = {}
         for m in range(2):
             for z in range(2):
-                raw = keep.tile([P, PACK, P], F32, name="w_raw%d%d" % (z, m), align_bytes=64)
+                raw = keep.tile([P, PACK, P], F32, name="w_raw%d%d" % (z, m), tag="w_raw%d%d" % (z, m), align_bytes=256)
                 nc.sync.dma_start(raw[:], w_rows[z, :, :, m * P : (m + 1) * P])
                 w_raw[z, m] = raw[:]
-        frac_sb = keep.tile([P, V], F32, name="frac_sb")
+        frac_sb = keep.tile([P, V], F32, name="frac_sb", align_bytes=256)
         nc.sync.dma_start(frac_sb[:], frac)
         nc.sync.dma_start(left_sb[:], left)
         nc.sync.dma_start(right_sb[:], right)
 
-        picked = [keep.tile([P, PACK, S], F32, name="picked%d" % z, align_bytes=64) for z in range(2)]
+        x_bf = [keep.tile([P, S * PACK], BF16, name="x_bf%d" % z, align_bytes=64) for z in range(2)]
 
         def scalar_gather(dst, src):
             nc.scalar.activation(dst, src, ACT.Copy)
 
-        def pick(copy, z, j, first, last):
-            copy(picked[z][:, j, first:last], plane[z, j].indirect(offs_sb[:, first // 16 : last // 16]))
+        def pick(copy, window, z, j, first, last):
+            copy(x_bf[z][:, PACK * first + j : PACK * last : PACK], window.indirect(offs_sb[:, first // 16 : last // 16]))
 
         def lay(copy, name, src):
-            grouped = keep.tile([P, src.shape[2], PACK], BF16, name=name, align_bytes=64)
+            grouped = keep.tile([P, P, PACK], BF16, name=name, align_bytes=64)
             interleave(copy, grouped[:], src)
-            return grouped[:]
+            return grouped[:].rearrange("p c t -> p (c t)")
 
         def quantize(name, grouped):
-            n = grouped.shape[1]
+            n = grouped.shape[1] // PACK
             words = keep.tile([P, n], U32, name=name + "_words", align_bytes=64)
             scales = keep.tile([P, n], U8, name=name + "_scales", align_bytes=64)
-            nc.vector.quantize_mx(
-                out=words[:].bitcast(FP8X4), scales=scales[:], in_=grouped.rearrange("p c t -> p (c t)")
-            )
+            nc.vector.quantize_mx(out=words[:].bitcast(FP8X4), scales=scales[:], in_=grouped)
             return words[:], scales[:]
 
         x_mx = {}
         w_mx = {}
 
-        for j in range(PACK):
-            pick(nc.vector.tensor_copy if j % 2 else scalar_gather, 0, j, 0, S)
-        laid = [lay(nc.vector.tensor_copy, "x_bf0%d" % h, picked[0][:, :, h * HALF : (h + 1) * HALF]) for h in range(2)]
-        for h in range(2):
-            words, scales = quantize("x0%d" % h, laid[h])
-            for q in range(2):
-                cols = slice(q * QUARTER, (q + 1) * QUARTER)
-                x_mx[0, 2 * h + q] = (words[:, cols], scales[:, cols])
+        for j in range(2):
+            pick(scalar_gather, pair[j][:], 0, j, 0, S)
+            pick(nc.vector.tensor_copy, pair[j][:, T:], 0, j + 2, 0, S)
+        words, scales = quantize("x0", x_bf[0][:])
+        for q in range(4):
+            cols = slice(q * QUARTER, (q + 1) * QUARTER)
+            x_mx[0, q] = (words[:, cols], scales[:, cols])
 
-        pick(scalar_gather, 1, 0, 0, S)
-        pick(scalar_gather, 1, 1, 0, S)
-        pick(scalar_gather, 1, 2, 0, THIRD_PLANE_CUT)
-        pick(nc.vector.tensor_copy, 1, 2, THIRD_PLANE_CUT, S)
-        pick(scalar_gather, 1, 3, 0, QUARTER)
-        pick(nc.vector.tensor_copy, 1, 3, LAST_PLANE_CUT, S)
-        pick(scalar_gather, 1, 3, QUARTER, LAST_PLANE_CUT)
+        for j in range(PACK):
+            cut = EARLY_CUT if j < 2 else LATE_CUT
+            pick(nc.vector.tensor_copy, plane[j][:], 1, j, 0, cut)
+            pick(scalar_gather, plane[j][:], 1, j, cut, S)
 
         y = [keep.tile([P, S], F32, name="y%d" % m) for m in range(2)]
         acc = {(m, q): psum.tile([P, QUARTER], F32, name="acc%d%d" % (m, q)) for m in range(2) for q in range(4)}
 
-        def products(z, m, quarters):
-            for q in quarters:
+        def products(z, m):
+            for q in QUARTER_ORDER:
                 nc.tensor.matmul_mx(
                     out=acc[m, q][:],
                     lhsT=w_mx[z, m][0].bitcast(FP8X4),
@@ -126,45 +118,47 @@ def tile_picked_lerp_gelu_e_kernel(tc, xT, w1, frac, offs, left, right, out):
                     stop=(z == 1),
                 )
 
-        def gelus(m, quarters):
-            for q in quarters:
+        def gelus(m):
+            for q in QUARTER_ORDER:
                 nc.scalar.activation(y[m][:, q * QUARTER : (q + 1) * QUARTER], acc[m, q][:], ACT.Gelu_apprx_tanh)
 
-        def lay_quarter(copy, q):
-            return lay(copy, "x_bf1%d" % q, picked[1][:, :, q * QUARTER : (q + 1) * QUARTER])
+        def quantize_quarter(q):
+            x_mx[1, q] = quantize("x1%d" % q, x_bf[1][:, q * QUARTER * PACK : (q + 1) * QUARTER * PACK])
 
-        x_bf = {0: lay_quarter(nc.vector.tensor_copy, 0), 3: lay_quarter(nc.scalar.copy, 3)}
-        w_bf00 = lay(nc.vector.tensor_copy, "w_bf00", w_raw[0, 0])
-        x_bf[1] = lay_quarter(nc.vector.tensor_copy, 1)
-        w_mx[0, 0] = quantize("w00", w_bf00)
-        products(0, 0, QUARTER_ORDER)
-        x_bf[2] = lay_quarter(nc.vector.tensor_copy, 2)
+        w_bf00 = lay(nc.scalar.copy, "w_bf00", w_raw[0, 0])
         w_bf10 = lay(nc.scalar.copy, "w_bf10", w_raw[1, 0])
-        x_mx[1, 0] = quantize("x10", x_bf[0])
-        w_mx[1, 0] = quantize("w10", w_bf10)
         w_bf01 = lay(nc.scalar.copy, "w_bf01", w_raw[0, 1])
-        for q in QUARTER_ORDER[1:]:
-            x_mx[1, q] = quantize("x1%d" % q, x_bf[q])
+        quantize_quarter(3)
+        w_mx[0, 0] = quantize("w00", w_bf00)
+        products(0, 0)
+        words = keep.tile([P, 3 * QUARTER], U32, name="x1_words", tag="w_raw00", align_bytes=256)
+        scales = keep.tile([P, 3 * QUARTER], U8, name="x1_scales", align_bytes=64)
+        for q in range(3):
+            cols = slice(q * QUARTER, (q + 1) * QUARTER)
+            nc.vector.quantize_mx(
+                out=words[:, cols].bitcast(FP8X4),
+                scales=scales[:, cols],
+                in_=x_bf[1][:, q * QUARTER * PACK : (q + 1) * QUARTER * PACK],
+            )
+            x_mx[1, q] = (words[:, cols], scales[:, cols])
+        w_mx[1, 0] = quantize("w10", w_bf10)
+        products(1, 0)
         w_mx[0, 1] = quantize("w01", w_bf01)
+        products(0, 1)
 
-        w_bf11 = keep.tile([P, P, PACK], BF16, name="w_bf11", align_bytes=64)
-        interleave(nc.vector.tensor_copy, w_bf11[:, :VECTOR_COLUMNS, :], w_raw[1, 1][:, :, :VECTOR_COLUMNS])
-        interleave(nc.scalar.copy, w_bf11[:, VECTOR_COLUMNS:, :], w_raw[1, 1][:, :, VECTOR_COLUMNS:])
-        for pair in (QUARTER_ORDER[:2], QUARTER_ORDER[2:]):
-            products(1, 0, pair)
-            gelus(0, pair)
+        w_bf11 = lay(nc.vector.tensor_copy, "w_bf11", w_raw[1, 1])
+        gelus(0)
         rest = keep.tile([P, V], F32, name="rest")
         nc.vector.tensor_scalar(rest[:], frac_sb[:], -1.0, 1.0, ALU.mult, ALU.add)
-        w_mx[1, 1] = quantize("w11", w_bf11[:])
-        for z in range(2):
-            products(z, 1, QUARTER_ORDER)
+        w_mx[1, 1] = quantize("w11", w_bf11)
+        products(1, 1)
 
         from_right = [keep.tile([P, V], F32, name="from_right%d" % m) for m in range(2)]
         from_left = [keep.tile([P, V], F32, name="from_left%d" % m) for m in range(2)]
         result = [keep.tile([P, V], F32, name="result%d" % m) for m in range(2)]
         samples = [slice(h * P, (h + 1) * P) for h in range(2)]
 
-        gelus(1, QUARTER_ORDER)
+        gelus(1)
         nc.vector.tensor_tensor(from_left[0][:], y[0][:].indirect(left_sb[:]), rest[:], ALU.mult)
         nc.vector.tensor_tensor(from_right[0][:], y[0][:].indirect(right_sb[:]), frac_sb[:], ALU.mult)
         nc.vector.tensor_tensor(result[0][:], from_left[0][:], from_right[0][:], ALU.add)

@@ -7,6 +7,7 @@ FLOPS = 2 * K * S * N
 
 F32 = mybir.dt.float32
 BF16 = mybir.dt.bfloat16
+I32 = mybir.dt.int32
 U32 = mybir.dt.uint32
 U16 = mybir.dt.uint16
 U8 = mybir.dt.uint8
@@ -18,7 +19,7 @@ P = 128
 PACK = 4
 HALF = S // 2
 QUARTER = S // 4
-EARLY_CUT = 192
+EARLY_CUT = 128
 LATE_CUT = 320
 QUARTER_ORDER = (3, 0, 1, 2)
 
@@ -90,13 +91,22 @@ def tile_picked_lerp_gelu_e_kernel(tc, xT, w1, frac, offs, left, right, out):
         x_mx = {}
         w_mx = {}
 
+        pairs = [keep.tile([P, 2, 2 * HALF], BF16, name="pairs%d" % h, align_bytes=64) for h in range(2)]
         for j in range(2):
-            pick(scalar_gather, pair[j][:], 0, j, 0, S)
-            pick(nc.vector.tensor_copy, pair[j][:, T:], 0, j + 2, 0, S)
-        words, scales = quantize("x0", x_bf[0][:])
-        for q in range(4):
-            cols = slice(q * QUARTER, (q + 1) * QUARTER)
-            x_mx[0, q] = (words[:, cols], scales[:, cols])
+            for h in range(2):
+                offsets = offs_sb[:, h * HALF // 16 : (h + 1) * HALF // 16]
+                scalar_gather(pairs[h][:, 0, j::2], pair[j][:].indirect(offsets))
+                nc.vector.tensor_copy(pairs[h][:, 1, j::2], pair[j][:, T:].indirect(offsets))
+        for h in range(2):
+            nc.vector.tensor_copy(
+                x_bf[0][:, h * HALF * PACK : (h + 1) * HALF * PACK].bitcast(I32).rearrange("p (c u) -> p c u", u=2),
+                pairs[h][:].bitcast(I32).rearrange("p u c -> p c u"),
+            )
+        for h in range(2):
+            words, scales = quantize("x0%d" % h, x_bf[0][:, h * HALF * PACK : (h + 1) * HALF * PACK])
+            for q in range(2):
+                cols = slice(q * QUARTER, (q + 1) * QUARTER)
+                x_mx[0, 2 * h + q] = (words[:, cols], scales[:, cols])
 
         for j in range(PACK):
             cut = EARLY_CUT if j < 2 else LATE_CUT

@@ -19,9 +19,8 @@ P = 128
 PACK = 4
 HALF = S // 2
 QUARTER = S // 4
-EARLY_CUT = 128
-LATE_CUT = 320
-QUARTER_ORDER = (3, 0, 1, 2)
+CUT = 192
+VECTOR_COLUMNS = 48
 
 
 def interleave(copy, dst, src):
@@ -109,15 +108,14 @@ def tile_picked_lerp_gelu_e_kernel(tc, xT, w1, frac, offs, left, right, out):
                 x_mx[0, 2 * h + q] = (words[:, cols], scales[:, cols])
 
         for j in range(PACK):
-            cut = EARLY_CUT if j < 2 else LATE_CUT
-            pick(nc.vector.tensor_copy, plane[j][:], 1, j, 0, cut)
-            pick(scalar_gather, plane[j][:], 1, j, cut, S)
+            pick(nc.vector.tensor_copy, plane[j][:], 1, j, 0, CUT)
+            pick(scalar_gather, plane[j][:], 1, j, CUT, S)
 
         y = [keep.tile([P, S], F32, name="y%d" % m) for m in range(2)]
         acc = {(m, q): psum.tile([P, QUARTER], F32, name="acc%d%d" % (m, q)) for m in range(2) for q in range(4)}
 
         def products(z, m):
-            for q in QUARTER_ORDER:
+            for q in range(4):
                 nc.tensor.matmul_mx(
                     out=acc[m, q][:],
                     lhsT=w_mx[z, m][0].bitcast(FP8X4),
@@ -129,29 +127,34 @@ def tile_picked_lerp_gelu_e_kernel(tc, xT, w1, frac, offs, left, right, out):
                 )
 
         def gelus(m):
-            for q in QUARTER_ORDER:
+            for q in range(4):
                 nc.scalar.activation(y[m][:, q * QUARTER : (q + 1) * QUARTER], acc[m, q][:], ACT.Gelu_apprx_tanh)
 
-        def quantize_quarter(q):
-            x_mx[1, q] = quantize("x1%d" % q, x_bf[1][:, q * QUARTER * PACK : (q + 1) * QUARTER * PACK])
-
-        w_bf00 = lay(nc.scalar.copy, "w_bf00", w_raw[0, 0])
-        w_bf10 = lay(nc.scalar.copy, "w_bf10", w_raw[1, 0])
+        w_bf00 = lay(nc.vector.tensor_copy, "w_bf00", w_raw[0, 0])
+        w_bf10 = keep.tile([P, P, PACK], BF16, name="w_bf10", align_bytes=64)
+        interleave(nc.scalar.copy, w_bf10[:, VECTOR_COLUMNS:, :], w_raw[1, 0][:, :, VECTOR_COLUMNS:])
         w_bf01 = lay(nc.scalar.copy, "w_bf01", w_raw[0, 1])
-        quantize_quarter(3)
         w_mx[0, 0] = quantize("w00", w_bf00)
         products(0, 0)
-        words = keep.tile([P, 3 * QUARTER], U32, name="x1_words", tag="w_raw00", align_bytes=256)
-        scales = keep.tile([P, 3 * QUARTER], U8, name="x1_scales", align_bytes=64)
-        for q in range(3):
-            cols = slice(q * QUARTER, (q + 1) * QUARTER)
-            nc.vector.quantize_mx(
-                out=words[:, cols].bitcast(FP8X4),
-                scales=scales[:, cols],
-                in_=x_bf[1][:, q * QUARTER * PACK : (q + 1) * QUARTER * PACK],
-            )
-            x_mx[1, q] = (words[:, cols], scales[:, cols])
-        w_mx[1, 0] = quantize("w10", w_bf10)
+        scales = keep.tile([P, S], U8, name="x1_scales", align_bytes=64)
+
+        def quantize_quarters(first, last, tag):
+            words = keep.tile([P, (last - first) * QUARTER], U32, name="x1_words%d" % first, tag=tag, align_bytes=256)
+            for q in range(first, last):
+                x_mx[1, q] = (
+                    words[:, (q - first) * QUARTER : (q - first + 1) * QUARTER],
+                    scales[:, q * QUARTER : (q + 1) * QUARTER],
+                )
+                nc.vector.quantize_mx(
+                    out=x_mx[1, q][0].bitcast(FP8X4),
+                    scales=x_mx[1, q][1],
+                    in_=x_bf[1][:, q * QUARTER * PACK : (q + 1) * QUARTER * PACK],
+                )
+
+        interleave(nc.vector.tensor_copy, w_bf10[:, :VECTOR_COLUMNS, :], w_raw[1, 0][:, :, :VECTOR_COLUMNS])
+        quantize_quarters(0, 2, "w_raw00")
+        w_mx[1, 0] = quantize("w10", w_bf10[:].rearrange("p c t -> p (c t)"))
+        quantize_quarters(2, 4, "w_raw10")
         products(1, 0)
         w_mx[0, 1] = quantize("w01", w_bf01)
         products(0, 1)

from contextlib import ExitStack

import concourse.mybir as mybir

K, T, S, V, N = 1024, 1024, 512, 256, 256
FLOPS = 2 * K * S * N

F32 = mybir.dt.float32
BF16 = mybir.dt.bfloat16
I32 = mybir.dt.int32
U32 = mybir.dt.uint32
U16 = mybir.dt.uint16
U8 = mybir.dt.uint8
FP8X4 = mybir.dt.float8_e4m3fn_x4
ACT = mybir.ActivationFunctionType
ALU = mybir.AluOpType

P = 128
PACK = 4
HALF = S // 2
QUARTER = S // 4
CUT = 192
VECTOR_COLUMNS = 48


def interleave(copy, dst, src):
    copy(dst.rearrange("p (c i) t -> p c t i", i=4), src.rearrange("p t (c i) -> p c t i", i=4))


def tile_picked_lerp_gelu_e_kernel(tc, xT, w1, frac, offs, left, right, out):
    nc = tc.nc
    with ExitStack() as ctx:
        keep = ctx.enter_context(tc.tile_pool(name="keep", bufs=1))
        psum = ctx.enter_context(tc.psum_pool(name="psum", bufs=1))

        offs_sb = keep.tile([P, S // 16], U16, name="offs_sb")
        left_sb = keep.tile([P, V // 16], U16, name="left_sb")
        right_sb = keep.tile([P, V // 16], U16, name="right_sb")

        warm = keep.tile([P, 8], F32, name="warm")
        warm_out = keep.tile([P, 8], F32, name="warm_out")
        nc.vector.memset(warm[:], 0.0)
        nc.scalar.activation(warm_out[:], warm[:], ACT.Gelu_apprx_tanh)

        x_rows = xT.rearrange("(z p j) t -> z p j t", p=P, j=PACK)
        pair = []
        for j in range(2):
            raw = keep.tile([P, 2 * T], F32, name="pair%d" % j, align_bytes=256)
            nc.sync.dma_start(raw[:].rearrange("p (u t) -> p u t", u=2), x_rows[0, :, j:PACK:2, :])
            pair.append(raw)
            if j == 0:
                nc.sync.dma_start(offs_sb[:], offs)
        plane = []
        for j in range(PACK):
            raw = keep.tile([P, T], F32, name="plane%d" % j, align_bytes=256)
            nc.sync.dma_start(raw[:], x_rows[1, :, j, :])
            plane.append(raw)
        w_rows = w1.rearrange("(z p j) m -> z p j m", p=P, j=PACK)
        w_raw = {}
        for m in range(2):
            for z in range(2):
                raw = keep.tile([P, PACK, P], F32, name="w_raw%d%d" % (z, m), tag="w_raw%d%d" % (z, m), align_bytes=256)
                nc.sync.dma_start(raw[:], w_rows[z, :, :, m * P : (m + 1) * P])
                w_raw[z, m] = raw[:]
        frac_sb = keep.tile([P, V], F32, name="frac_sb", align_bytes=256)
        nc.sync.dma_start(frac_sb[:], frac)
        nc.sync.dma_start(left_sb[:], left)
        nc.sync.dma_start(right_sb[:], right)

        x_bf = [keep.tile([P, S * PACK], BF16, name="x_bf%d" % z, align_bytes=64) for z in range(2)]

        def scalar_gather(dst, src):
            nc.scalar.activation(dst, src, ACT.Copy)

        def pick(copy, window, z, j, first, last):
            copy(x_bf[z][:, PACK * first + j : PACK * last : PACK], window.indirect(offs_sb[:, first // 16 : last // 16]))

        def lay(copy, name, src):
            grouped = keep.tile([P, P, PACK], BF16, name=name, align_bytes=64)
            interleave(copy, grouped[:], src)
            return grouped[:].rearrange("p c t -> p (c t)")

        def quantize(name, grouped):
            n = grouped.shape[1] // PACK
            words = keep.tile([P, n], U32, name=name + "_words", align_bytes=64)
            scales = keep.tile([P, n], U8, name=name + "_scales", align_bytes=64)
            nc.vector.quantize_mx(out=words[:].bitcast(FP8X4), scales=scales[:], in_=grouped)
            return words[:], scales[:]

        x_mx = {}
        w_mx = {}

        pairs = [keep.tile([P, 2, 2 * HALF], BF16, name="pairs%d" % h, align_bytes=64) for h in range(2)]
        for j in range(2):
            for h in range(2):
                offsets = offs_sb[:, h * HALF // 16 : (h + 1) * HALF // 16]
                scalar_gather(pairs[h][:, 0, j::2], pair[j][:].indirect(offsets))
                nc.vector.tensor_copy(pairs[h][:, 1, j::2], pair[j][:, T:].indirect(offsets))
        for h in range(2):
            nc.vector.tensor_copy(
                x_bf[0][:, h * HALF * PACK : (h + 1) * HALF * PACK].bitcast(I32).rearrange("p (c u) -> p c u", u=2),
                pairs[h][:].bitcast(I32).rearrange("p u c -> p c u"),
            )
        for h in range(2):
            words, scales = quantize("x0%d" % h, x_bf[0][:, h * HALF * PACK : (h + 1) * HALF * PACK])
            for q in range(2):
                cols = slice(q * QUARTER, (q + 1) * QUARTER)
                x_mx[0, 2 * h + q] = (words[:, cols], scales[:, cols])

        for j in range(PACK):
            pick(nc.vector.tensor_copy, plane[j][:], 1, j, 0, CUT)
            pick(scalar_gather, plane[j][:], 1, j, CUT, S)

        y = [keep.tile([P, S], F32, name="y%d" % m) for m in range(2)]
        acc = {(m, q): psum.tile([P, QUARTER], F32, name="acc%d%d" % (m, q)) for m in range(2) for q in range(4)}

        def products(z, m):
            for q in range(4):
                nc.tensor.matmul_mx(
                    out=acc[m, q][:],
                    lhsT=w_mx[z, m][0].bitcast(FP8X4),
                    lhsT_scale=w_mx[z, m][1],
                    rhs=x_mx[z, q][0].bitcast(FP8X4),
                    rhs_scale=x_mx[z, q][1],
                    start=(z == 0),
                    stop=(z == 1),
                )

        def gelus(m):
            for q in range(4):
                nc.scalar.activation(y[m][:, q * QUARTER : (q + 1) * QUARTER], acc[m, q][:], ACT.Gelu_apprx_tanh)

        w_bf00 = lay(nc.vector.tensor_copy, "w_bf00", w_raw[0, 0])
        w_bf10 = keep.tile([P, P, PACK], BF16, name="w_bf10", align_bytes=64)
        interleave(nc.scalar.copy, w_bf10[:, VECTOR_COLUMNS:, :], w_raw[1, 0][:, :, VECTOR_COLUMNS:])
        w_bf01 = lay(nc.scalar.copy, "w_bf01", w_raw[0, 1])
        w_mx[0, 0] = quantize("w00", w_bf00)
        products(0, 0)
        scales = keep.tile([P, S], U8, name="x1_scales", align_bytes=64)

        def quantize_quarters(first, last, tag):
            words = keep.tile([P, (last - first) * QUARTER], U32, name="x1_words%d" % first, tag=tag, align_bytes=256)
            for q in range(first, last):
                x_mx[1, q] = (
                    words[:, (q - first) * QUARTER : (q - first + 1) * QUARTER],
                    scales[:, q * QUARTER : (q + 1) * QUARTER],
                )
                nc.vector.quantize_mx(
                    out=x_mx[1, q][0].bitcast(FP8X4),
                    scales=x_mx[1, q][1],
                    in_=x_bf[1][:, q * QUARTER * PACK : (q + 1) * QUARTER * PACK],
                )

        interleave(nc.vector.tensor_copy, w_bf10[:, :VECTOR_COLUMNS, :], w_raw[1, 0][:, :, :VECTOR_COLUMNS])
        quantize_quarters(0, 2, "w_raw00")
        w_mx[1, 0] = quantize("w10", w_bf10[:].rearrange("p c t -> p (c t)"))
        quantize_quarters(2, 4, "w_raw10")
        products(1, 0)
        w_mx[0, 1] = quantize("w01", w_bf01)
        products(0, 1)

        w_bf11 = lay(nc.vector.tensor_copy, "w_bf11", w_raw[1, 1])
        gelus(0)
        rest = keep.tile([P, V], F32, name="rest")
        nc.vector.tensor_scalar(rest[:], frac_sb[:], -1.0, 1.0, ALU.mult, ALU.add)
        w_mx[1, 1] = quantize("w11", w_bf11)
        products(1, 1)

        from_right = [keep.tile([P, V], F32, name="from_right%d" % m) for m in range(2)]
        from_left = [keep.tile([P, V], F32, name="from_left%d" % m) for m in range(2)]
        result = [keep.tile([P, V], F32, name="result%d" % m) for m in range(2)]
        samples = [slice(h * P, (h + 1) * P) for h in range(2)]

        gelus(1)
        nc.vector.tensor_tensor(from_left[0][:], y[0][:].indirect(left_sb[:]), rest[:], ALU.mult)
        nc.vector.tensor_tensor(from_right[0][:], y[0][:].indirect(right_sb[:]), frac_sb[:], ALU.mult)
        nc.vector.tensor_tensor(result[0][:], from_left[0][:], from_right[0][:], ALU.add)
        nc.sync.dma_start(out[0:P, :], result[0][:])
        fetched = [keep.tile([P, P], F32, name="left_1%d" % h) for h in range(2)]
        for h in range(2):
            scalar_gather(fetched[h][:], y[1][:].indirect(left_sb[:, h * (P // 16) : (h + 1) * (P // 16)]))
        nc.vector.tensor_tensor(from_right[1][:], y[1][:].indirect(right_sb[:]), frac_sb[:], ALU.mult)
        for h in range(2):
            nc.vector.tensor_tensor(from_left[1][:, samples[h]], fetched[h][:], rest[:, samples[h]], ALU.mult)
        for cols in samples:
            nc.vector.tensor_tensor(result[1][:, cols], from_left[1][:, cols], from_right[1][:, cols], ALU.add)
        nc.sync.dma_start(out[P:N, :], result[1][:])
